import numpy as np, ml_dtypes
CORES = [16,17,18,19,32,33,34,35]
N = 8
BF = ml_dtypes.bfloat16
NL, W, B, RO, Q = 116, 3712, 160, 4, 4
def parts(rng):
    X = rng.integers(0, 256, (N, 8, 16, W)); L = rng.integers(0, W, (N, 8, 16, W))
    y = (rng.integers(0, 256, (N, 8, 16, B)) * rng.integers(1, 9, (N, 8, 1, B))) >> 3
    return X, L, y, rng.integers(0, NL, (N, 8, B)), rng.integers(0, 4096, (N, 8, B))
def pack(X, L, y, ln, T):
    return {"xw": np.ascontiguousarray(X.reshape(N, 128, W)).astype(np.float32).astype(BF), "il": np.ascontiguousarray(L.reshape(N, 128, W)).astype(np.int32),
            "y0": np.ascontiguousarray(y.reshape(N, 128, B)).astype(np.float32).astype(BF), "ln0": np.ascontiguousarray(ln).astype(np.int32), "tk0": np.ascontiguousarray(T).astype(np.int32)}
def setup_inputs(rng):
    return pack(*parts(rng))
def setup_inputs_spread(rng):
    X = rng.integers(0, 256, (N, 8, 16, W)) >> rng.integers(0, 9, (N, 8, 1, W)); y = rng.integers(0, 256, (N, 8, 16, B)) >> rng.integers(0, 9, (N, 8, 1, B))
    a = np.exp2(rng.integers(-2, 3, (N, 8, 16, 1))); b = np.exp2(rng.integers(-2, 3, (N, 8, 16, 1)))
    line = np.minimum((NL * rng.random((N, 8, 16, W)) ** a).astype(np.int64), NL - 1); wait = np.minimum((32 * rng.random((N, 8, 16, W)) ** b).astype(np.int64), 31)
    ln = np.minimum((NL * rng.random((N, 8, B)) ** 3).astype(np.int64), NL - 1); T = np.minimum(np.exp2(12 * rng.random((N, 8, B))).astype(np.int64) - 1, 4095)
    return pack(X, 32 * line + wait, y, ln, T)
def ends(rng, top, *shape):
    k = rng.integers(0, 4, shape[:-2] + (1, shape[-1]))
    return top * np.where(k < 2, k, rng.integers(0, 2, shape))
def setup_inputs_ends(rng):
    X = ends(rng, 255, N, 8, 16, W); y = ends(rng, 255, N, 8, 16, B)
    L = np.where(rng.random((N, 8, 16, W)) < 0.8, ends(rng, W - 1, N, 8, 16, W), rng.integers(0, W, (N, 8, 16, W)))
    ln = (NL - 1) * rng.integers(0, 2, (N, 8, B)); T = 4095 * rng.integers(0, 2, (N, 8, B))
    L[..., 0] = 0; L[:, :, 1, 0] = W - 1; L[..., 31] = (W - 1) * rng.integers(0, 2, (N, 8, 16))
    L[..., W - 32] = W - 1; L[:, :, 0, W - 32] = 0; L[..., W - 1] = W - 1; L[:, :, 0, W - 1] = 0
    X[..., 0] = 0; X[..., W - 1] = 0; X[..., W - 2] = 255
    for q in range(N):
        if q == 1:
            for c in (0, 31, W - 2, W - 1): X[q, :, :, c] = 255
            y[q] = np.where(np.argsort(rng.random((8, 16, B)), axis=1) < rng.integers(0, 9, (8, 1, B)), 0, 255)
        else:
            if q == N - 1: y[q] = 0
            for i, l, t, v in ((0, NL - 1, 4095, 0), (B - 1, NL - 1, 4095, 0), (B - 2, NL - 1, 4095, 255), (1, NL - 1, 0, 255), (B - 4, NL - 1, 0, 255), (3, 0, 0, 0), (B - 3, 0, 0, 0)):
                ln[q, :, i] = l; T[q, :, i] = t; y[q, :, :, i] = v
            if q == N - 1: y[q, :7, :, B - 2] = 0
            if q == 2: y[q] = np.where(np.argsort(rng.random((8, 16, B)), axis=1) < rng.integers(9, 17, (8, 1, B)), 0, 255)
    return pack(X, L, y, ln, T)
def setup_inputs_corners(rng):
    X, L, y, ln, T = parts(rng)
    T = np.where(rng.random(T.shape) < 0.7, rng.choice(np.array([0, 15, 16, 31, 32, 4064, 4080, 4095]), T.shape), T)
    ln = np.where(rng.random(ln.shape) < 0.4, rng.choice(np.array([0, NL - 1]), ln.shape), ln)
    for q in range(N):
        for g in range(8):
            e = (q + g) % 8
            if e == 0: ln[q, g] = ln[q, g, 0]; T[q, g] = T[q, g, B - 1]
            elif e == 1: L[q, g] = np.arange(W)
            elif e == 2: L[q, g] = 0
            elif e == 3: L[q, g] = W - 1
            elif e == 4: X[q, g] = np.maximum(X[q, g], 1); y[q, g] = np.where(np.argsort(rng.random((16, B)), axis=0) < rng.integers(8, 10, (1, B)), 0, 255)
            elif e == 5: X[q, g] = 0
            elif e == 6: X[q, g] = 255; y[q, g] = rng.integers(128, 256, (16, B))
            else:
                a = rng.permutation(W)[:B]; ln[q, g] = a >> 5; T[q, g] = (a & 31) + 32 * rng.integers(0, 128, B); h = B // 4
                pl = np.concatenate([np.array([0, W - 1]), 1 + rng.permutation(W - 2)])
                d = rng.permutation(np.concatenate([pl[:h], pl[:h], pl[h:B - h]]))
                L[q, g, 15, a] = (d & 4064) + ((d - T[q, g]) & 31)
    return pack(X, L, y, ln, T)
def setup_inputs_crowd(rng):
    X, L, y, ln, T = parts(rng)
    few = rng.integers(0, NL, (N, 8, 1, 4)); few[:, ::2, :, 0] = NL - 1; few[:, 1::2, :, 1] = 0
    L[:, :, 0:2] = (L[:, :, 0:2] & 31) + 32 * np.take_along_axis(few, rng.integers(0, 4, (N, 8, 1, 2 * W)), 3).reshape(N, 8, 2, W)
    L[:, :, 15:16] = (L[:, :, 15:16] & 31) + 32 * np.take_along_axis(few, rng.integers(0, 2, (N, 8, 1, W)), 3)
    ln = np.take_along_axis(few, rng.integers(0, 4, (N, 8, 1, B)), 3).reshape(N, 8, B)
    p = int(rng.integers(0, N)); q = (p + 1) % N
    X[p] = 0; y[p] = 255 - (rng.integers(0, 128, (8, 16, B)) >> (3 * rng.integers(0, 2, (8, 1, B))))
    X[q] = np.maximum(X[q], 1); y[q] = rng.integers(128, 256, (8, 16, B))
    y[q, int(rng.integers(0, 8)), :, rng.permutation(B)[:int(rng.integers(1, 32))]] = 0
    return pack(X, L, y, ln, T)
def check_inputs(d):
    bad = []
    for k, hi in (("xw", 255), ("il", W - 1), ("y0", 255), ("ln0", NL - 1), ("tk0", 4095)):
        v = np.asarray(d[k]).astype(np.float64)
        if not np.all((v >= 0) & (v <= hi)): bad.append("range of " + k)
        elif not np.all(v == np.floor(v)): bad.append("whole numbers of " + k)
    return bad
def reference(xw, il, y0, ln0, tk0):
    X = xw.astype(np.float32).astype(np.int64).reshape(N, 8, 16, W); L = il.astype(np.int64).reshape(N, 8, 16, W)
    y = y0.astype(np.float32).astype(np.int64).reshape(N, 8, 16, B); ln = ln0.astype(np.int64); T = tk0.astype(np.int64)
    A = np.zeros(N, np.int64)
    for step in range(RO):
        a = 32 * ln + (T & 31)
        c = np.take_along_axis(L, a[:, :, None, :], 3)
        s = (c & 4064) + ((c + T[:, :, None, :]) & 31)
        v = np.take_along_axis(X, np.ascontiguousarray(s.transpose(0, 1, 3, 2)).reshape(N, 8, 1, 16 * B), 3).reshape(N, 8, 16, B, 16 // Q, Q)
        m = np.max(np.min(v, axis=-1), axis=-1)
        z = np.abs(m - y)
        skip = np.add.reduce((z >= y).astype(np.int64), axis=2) >= 9
        ln = np.where(skip, c[:, :, 1], c[:, :, 0]) >> 5
        d = s[:, :, 15]
        T = (T + 1 + (np.add.reduce(z, axis=2) & 31) + (A & 31)[:, None, None]) & 4095
        A = np.add.reduce(skip.reshape(N, 8 * B).astype(np.int64), axis=1)
        y = np.roll(z, 1, axis=0); ln = np.roll(ln, 1, axis=0); T = np.roll(T, 1, axis=0); d = np.roll(d, 1, axis=0)
        for q in range(N):
            for g in range(8):
                p, first = np.unique(d[q, g], return_index=True)
                u = L[q, g]; o = u[:, p]
                u[:, p] = (o & 4064) + ((o + y[q, g][:, first]) & 31)
        if step < RO - 1:
            np.put_along_axis(X, (16 * np.arange(B) + (T & 15))[:, :, None, :], y, 3)
    return {"yw": (L & 31).reshape(N, 128, W).astype(np.float32).astype(BF), "yy": y.reshape(N, 128, B).astype(np.float32).astype(BF), "yl": ln.astype(np.float32), "yt": T.astype(np.float32)}

@@ -1,0 +1,458 @@
+from concourse.mybir import AluOpType, AxisListType, ActivationFunctionType
+
+W, B, RO = 3712, 160, 4
+UN = 464
+SCH = [(0, 56), (56, 112), (112, 144), (144, 160)]
+OFF = 4352.0
+OFD = OFF - 16.0
+M32 = 402653184.0
+M16 = 201326592.0
+M16K = 1.5 * 2.0 ** 37
+AC = (17.0 - 15.5, 17.0, 17.0 - 7.5)
+
+SCRATCH = {
+    "ilt": ("sbuf", [128, W], "int32"), "tmp": ("sbuf", [128, W], "int32"),
+    "xt": ("sbuf", [128, W], "bfloat16"), "wy": ("sbuf", [128, W + B], "bfloat16"),
+    "colt": ("sbuf", [128, W], "bfloat16"),
+    "vv": ("sbuf", [128, 16 * B], "bfloat16"), "mn": ("sbuf", [128, 16 * B], "bfloat16"), "mx": ("sbuf", [128, 4 * B], "bfloat16"),
+    "eq": ("sbuf", [128, 10 * B], "bfloat16"), "dru": ("sbuf", [128, B], "uint16"),
+    "y0t": ("sbuf", [128, B], "bfloat16"),
+    "ln8": ("sbuf", [8, B], "int32"), "tk8": ("sbuf", [8, B], "int32"), "ti8": ("sbuf", [8, B], "int32"), "th8": ("sbuf", [8, B], "int32"),
+    "lb8": ("sbuf", [8, B], "bfloat16"), "tb8": ("sbuf", [8, B], "bfloat16"), "tc8": ("sbuf", [8, B], "bfloat16"),
+    "sel": ("sbuf", [8, 128], "bfloat16"), "sel32": ("sbuf", [8, 128], "bfloat16"), "tf0": ("sbuf", [128, 10], "float32"),
+    "ac": ("sbuf", [128, 3], "float32"), "awm0": ("sbuf", [128, 10], "float32"), "awm1": ("sbuf", [128, 10], "float32"), "thr": ("sbuf", [128, 10], "float32"),
+    "wg": ("sbuf", [128, B], "bfloat16"), "wgi": ("sbuf", [128, B], "int32"), "lg": ("sbuf", [128, B], "bfloat16"), "cg": ("sbuf", [128, B], "bfloat16"), "sg": ("sbuf", [128, B], "bfloat16"),
+    "st": ("sbuf", [128, B], "uint16"), "kk": ("sbuf", [128, B], "bfloat16"),
+    "ui": ("sbuf", [128, B], "int32"), "ui2": ("sbuf", [128, B], "int32"), "wold": ("sbuf", [128, B], "bfloat16"),
+    "dws": ("sbuf", [128, B], "float32"), "ps": ("sbuf", [128, B], "float32"), "rs": ("sbuf", [128, B], "float32"), "qs": ("sbuf", [128, B], "float32"),
+    "lose": ("sbuf", [128, 10], "float32"), "lose2": ("sbuf", [128, 10], "float32"), "dd": ("sbuf", [128, 10], "float32"),
+    "d0": ("sbuf", [128, 120], "float32"), "d1": ("sbuf", [128, 120], "float32"), "po": ("sbuf", [128, 120], "float32"),
+    "ta4": ("sbuf", [128, 10], "float32"),
+    "acol": ("sbuf", [128, 1], "float32"), "am1": ("sbuf", [128, 1], "float32"), "am2": ("sbuf", [128, 1], "float32"), "am3": ("sbuf", [128, 1], "float32"), "am": ("sbuf", [128, 2], "float32"),
+    "tfa": ("sbuf", [128, 10], "float32"), "qi": ("sbuf", [128, 10], "int32"), "qi2": ("sbuf", [128, 10], "int32"), "tfn": ("sbuf", [128, 10], "float32"),
+    "aw0": ("sbuf", [128, 10], "uint16"),
+    "fi": ("sbuf", [128, 20], "int32"), "fi2": ("sbuf", [128, 20], "int32"), "ft": ("sbuf", [128, 32], "float32"), "ftt": ("sbuf", [128, 32], "float32"),
+    "ones": ("sbuf", [128, 224], "bfloat16"), "g1": ("sbuf", [128, 128], "bfloat16"), "gb": ("sbuf", [128, 128], "bfloat16"), "i1": ("sbuf", [128, 128], "bfloat16"),
+    "i32": ("sbuf", [128, 128], "bfloat16"), "in1": ("sbuf", [128, 128], "bfloat16"),
+    "g8": ("sbuf", [128, 128], "bfloat16"), "gw": ("sbuf", [128, 128], "bfloat16"),
+    "e15": ("sbuf", [128, 128], "bfloat16"), "e15x": ("sbuf", [128, 128], "bfloat16"), "e15n": ("sbuf", [128, 128], "bfloat16"),
+    "ea": ("sbuf", [128, 128], "bfloat16"), "eb": ("sbuf", [128, 128], "bfloat16"), "one5": ("sbuf", [128, 128], "float32"),
+    "pq": ("sbuf", [128, B], "int32"), "pq2": ("sbuf", [128, B], "int32"), "mask": ("sbuf", [128, B], "bfloat16"), "q16": ("sbuf", [128, B], "float32"), "rsw": ("sbuf", [128, B], "float32"),
+    "rs1": ("sbuf", [128, 896], "bfloat16"), "rs2": ("sbuf", [128, 224], "bfloat16"),
+    "pm0": ("sbuf", [128, 10], "int32"), "pm": ("sbuf", [128, 10], "int32"), "c16": ("sbuf", [128, 10], "int32"),
+    "li": ("sbuf", [128, 10], "float32"), "li16": ("sbuf", [128, 10], "float32"), "dum": ("sbuf", [128, 10], "float32"),
+    "gwa": ("sbuf", [128, 1280], "bfloat16"), "e0": ("sbuf", [128, 128], "bfloat16"), "e0x": ("sbuf", [128, 128], "bfloat16"),
+    "half": ("sbuf", [128, 32], "float32"), "rv": ("sbuf", [128, 16], "float32"), "rv2": ("sbuf", [128, 16], "float32"), "rv3": ("sbuf", [128, 16], "float32"),
+    "y2": ("sbuf", [128, B], "bfloat16"), "kk2": ("sbuf", [128, B], "bfloat16"),
+}
+for _t in range(RO):
+    SCRATCH["m1_%d" % _t] = ("sbuf", [128, 20], "uint16")
+    SCRATCH["zs_%d" % _t] = ("sbuf", [128, B], "bfloat16")
+    SCRATCH["m3_%d" % _t] = ("sbuf", [128, 20], "uint16")
+    SCRATCH["r1_%d" % _t] = ("sbuf", [128, 20], "uint16")
+    SCRATCH["rz_%d" % _t] = ("sbuf", [128, B], "bfloat16")
+    SCRATCH["r3_%d" % _t] = ("sbuf", [128, 20], "uint16")
+for _t in range(8):
+    SCRATCH["b%d" % _t] = ("psum", [128, 512], "float32")
+SEMAPHORES = ["qV", "qS", "qT", "qP", "loc", "dil0", "dil1", "dx", "dy", "dln", "dtk", "oyy", "oyw", "osm", "osn"]
+SEMAPHORES += ["a%s_%d" % (m, t) for m in ("1", "z", "3") for t in range(RO)]
+
+
+def rank_program(g, core, T, topo):
+    rank = T.rank_of(core)
+    if rank is None:
+        return
+    n = len(T.cores)
+    nxt, prv = T.cores[(rank + 1) % n], T.cores[(rank - 1) % n]
+    OP, AF = AluOpType, ActivationFunctionType
+    ADD, SUB, MUL, MAX, MIN, EQ, GE, GT = OP.add, OP.subtract, OP.mult, OP.max, OP.min, OP.is_equal, OP.is_ge, OP.is_gt
+    AND, SHR = OP.bitwise_and, OP.arith_shift_right
+    eng = {"V": g.vector, "S": g.scalar, "T": g.tensor, "P": g, "Y": g.sync}
+    know = {e: {} for e in eng}
+    tot, lastw, readers = {}, {}, {}
+
+    def waits(e, r, w):
+        deps = []
+        for k in r:
+            deps += lastw.get(k, [])
+        for k in w:
+            deps += lastw.get(k, []) + readers.get(k, [])
+        deps = [d for d in deps if know[e].get(d[0], 0) < d[1] and not (e == "T" and d[0] == "qT")]
+        need = {}
+        for d in deps:
+            if d[0] not in need or need[d[0]][1] < d[1]:
+                need[d[0]] = d
+        keep = [d for d in need.values() if not any(o is not d and o[2].get(d[0], 0) >= d[1] for o in need.values())]
+        for d in keep:
+            eng[e].wait_ge(T.sem[d[0]], d[1])
+        for d in need.values():
+            for s, v in list(d[2].items()) + [(d[0], d[1])]:
+                know[e][s] = max(know[e].get(s, 0), v)
+
+    def done(e, inst, r, w, sem, inc):
+        tot[sem] = tot.get(sem, 0) + inc
+        inst.then_inc(T.sem[sem], inc)
+        snap = dict(know[e])
+        snap[sem] = tot[sem]
+        ev = (sem, tot[sem], snap)
+        for k in r:
+            readers.setdefault(k, []).append(ev)
+        for k in w:
+            lastw[k] = [ev]
+            readers[k] = []
+
+    def do(e, fn, r, w):
+        waits(e, r, w)
+        done(e, fn(eng[e]), r, w, "q" + e, 1)
+
+    def dma(e, out, in_, r, w, sem):
+        waits(e, r, w)
+        done(e, eng[e].dma_start(out, in_), r, w, sem, 16)
+
+    def tt(out, a, b, op, r, w):
+        do("V", lambda v: v.tensor_tensor(out, a, b, op), r, w)
+
+    def ts(out, a, s1, o1, r, w, s2=None, o2=None):
+        if o2 is None:
+            do("V", lambda v: v.tensor_scalar(out, a, s1, None, o1), r, w)
+        else:
+            do("V", lambda v: v.tensor_scalar(out, a, s1, s2, o1, o2), r, w)
+
+    def cp(out, a, r, w):
+        do("V", lambda v: v.tensor_copy(out, a), r, w)
+
+    def ms(ap, val, w):
+        do("V", lambda v: v.memset(ap, val), [], w)
+
+    def scan(out, x0, x1, o0, o1, r, w):
+        do("V", lambda v: v.tensor_tensor_scan(out, x0, x1, 0.0, o0, o1), r, w)
+
+    def mm(out, lhs, rhs, start, stop, r, w):
+        do("T", lambda v: v.matmul(out, lhs, rhs, start, stop), r, w)
+
+    def act(out, in_, func, r, w, bias=None, scale=None):
+        if scale is not None and bias is not None:
+            do("S", lambda v: v.activation(out, in_, func, bias=bias, scale=scale), r, w)
+        elif scale is not None:
+            do("S", lambda v: v.activation(out, in_, func, scale=scale), r, w)
+        elif bias is None:
+            do("S", lambda v: v.activation(out, in_, func), r, w)
+        else:
+            do("S", lambda v: v.activation(out, in_, func, bias=bias), r, w)
+
+    sent = [0]
+    rid, pid, _se = topo.addr(nxt)
+    msk, ne = topo.mask(core, nxt), len(topo.engines(core, nxt))
+    na = len(topo.engines(prv, core))
+
+    def send(out, in_, r, sem):
+        waits("P", r, [])
+        g.remote_dma(out, in_, T.sem[sem], T.sem.loc, pid, rid, msk)
+        sent[0] += ne
+
+    def arrives(tok, sem):
+        lastw[tok] = [(sem, na, {sem: na})]
+        tot[sem] = na
+
+    dma("Y", T.ln8[:], T.ln0[:], [], ["ln8"], "dln")
+    dma("Y", T.tk8[:], T.tk0[:], [], ["tk8"], "dtk")
+    for q in range(2):
+        c = q * 1856
+        dma("Y", T.ilt[:, c:c + 1856], T.il[:, c:c + 1856], [], ["il%d" % q], "dil%d" % q)
+    dma("Y", T.xt[:], T.xw[:], [], ["x"], "dx")
+    dma("S", T.y0t[:], T.y0[:], [], ["y0"], "dy")
+
+    def pool(fn, r, w):
+        do("P", fn, r, w)
+    ms(T.ones[:], 1.0, ["ones"])
+    pool(lambda p: p.iota(T.pq[:], [[0, 10], [1, 16]], 128, -1), [], ["pq"])
+    pool(lambda p: p.iota(T.q16[:], [[0, 10], [1, 16]], 0, 0, allow_small_or_imprecise_dtypes=True), [], ["q16"])
+    pool(lambda p: p.affine_select(T.i1[:], T.ones[:, 0:128], [[-1, 128]], EQ, 0.0, 0, 1), ["ones"], ["i1"])
+    pool(lambda p: p.affine_select(T.sel[:], T.ones[0:8, 0:128], [[1, 8], [0, 16]], EQ, 0.0, 0, -1), ["ones"], ["sel"])
+    pool(lambda p: p.iota(T.pm0[:], [[0, 10]], 0, 1), [], ["pm0"])
+    pool(lambda p: p.iota(T.c16[:], [[16, 10]], 0, 0), [], ["c16"])
+    pool(lambda p: p.iota(T.colt[:, 0:928], [[0, 29], [1, 32]], -16, 0, allow_small_or_imprecise_dtypes=True), [], ["colt0"])
+    pool(lambda p: p.affine_select(T.gb[:], T.ones[:, 0:128], [[-16, 8], [0, 16]], GE, 0.0, 0, 1), ["ones"], ["gb"])
+    pool(lambda p: p.affine_select(T.g1[:], T.gb[:], [[16, 8], [0, 16]], GE, 0.0, 15, -1), ["gb"], ["g1"])
+
+    def fill(ap, n_, v, w):
+        act(ap, T.ones[:, 0:n_], AF.Copy, ["ones"], [w], scale=v)
+    fill(T.half[:, 0:16], 16, 0.5, "half")
+    fill(T.half[:, 16:32], 16, 0.0, "half")
+    fill(T.d0[:], 120, 1.0, "d0c")
+    for lo, hi, v in ((0, 60, 0.0), (5, 60, -1.0), (60, 120, 0.0), (61, 120, 0.0), (62, 120, 0.0), (65, 120, -1.0)):
+        fill(T.d0[:, lo:hi:6], 10, v, "d0c")
+    fill(T.d1[:], 120, 0.0, "d1c")
+    for lo, hi, v in ((3, 60, M32), (4, 60, -M32), (63, 120, M16), (64, 120, -M16)):
+        fill(T.d1[:, lo:hi:6], 10, v, "d1c")
+    for k in ("d1b", "d1s", "d1x1", "d1x2", "d1x3", "d1x4"):
+        lastw[k] = lastw["d1c"]
+    lastw["d0s"] = lastw["d0c"]
+    fill(T.rs2[:], 224, 0.0, "rs2")
+    Q4 = [[0, 56], [1, 4]]
+    pool(lambda p: p.affine_select(T.rs1[:, 0:224], T.rs2[:], Q4, OP.not_equal, 512.0, 0, 0), ["rs2"], ["rs1_0"])
+    pool(lambda p: p.affine_select(T.rs2[:], T.rs2[:], Q4, EQ, 512.0, 0, 0), ["rs2"], ["rs2"])
+    CT = ["colt%d" % j for j in range(4)]
+
+    ts(T.pq2[:], T.pq[:], 15, AND, ["pq"], ["pq2"])
+    ts(T.mask[:], T.pq2[:], 0.0, GT, ["pq2"], ["mask"], -(2.0 ** 60), MUL)
+    ts(T.rsw[:], T.q16[:], -0.5, ADD, ["q16"], ["rsw"], 1e27, MUL)
+    act(T.sel32[:], T.sel[:], AF.Copy, ["sel"], ["sel32"], scale=32.0)
+    cp(T.lb8[:], T.ln8[:], ["ln8"], ["lb8"])
+    ts(T.ti8[:], T.tk8[:], 31, AND, ["tk8"], ["ti8"])
+    ts(T.th8[:], T.tk8[:], 5, SHR, ["tk8"], ["th8"])
+    cp(T.tb8[:], T.ti8[:], ["ti8"], ["tb8"])
+    cp(T.tc8[:], T.th8[:], ["th8"], ["tc8"])
+    for bb, tb, hi, thi in ((T.b0, "b0", T.lb8, "lb8"), (T.b1, "b1", T.tc8, "tc8")):
+        mm(bb[:, 0:B], T.i1[:], T.mask[:], True, False, ["i1", "mask"], [tb])
+        mm(bb[:, 0:B], T.sel32[:], hi[:], False, False, ["sel32", thi], [tb])
+        mm(bb[:, 0:B], T.sel[:], T.tb8[:], False, True, ["sel", "tb8"], [tb])
+    scan(T.qs[:], T.rsw[:], T.b0[:, 0:B], MIN, MAX, ["rsw", "b0"], ["qs"])
+    cp(T.aw0[:], T.qs[:, 15:B:16], ["qs"], ["aw_0"])
+    scan(T.ps[:], T.rsw[:], T.b1[:, 0:B], MIN, MAX, ["rsw", "b1"], ["ps"])
+    cp(T.tf0[:], T.ps[:, 15:B:16], ["ps"], ["tf0"])
+
+    GP = [[-16, 8], [0, 16]]
+    pool(lambda p: p.affine_select(T.e15[:], T.ones[:, 0:128], GP, EQ, 0.0, -15, 1), ["ones"], ["e15"])
+    pool(lambda p: p.affine_select(T.e0[:], T.ones[:, 0:128], GP, EQ, 0.0, 0, 1), ["ones"], ["e0"])
+    act(T.i32[:], T.i1[:], AF.Copy, ["i1"], ["i32"], scale=32.0)
+    act(T.in1[:], T.i1[:], AF.Copy, ["i1"], ["in1"], scale=-1.0)
+    for j in range(1, 4):
+        act(T.colt[:, 928 * j:928 * j + 928], T.colt[:, 0:928], AF.Copy, ["colt0"], ["colt%d" % j])
+    act(T.cg[:], T.colt[:].indirect(T.aw0[:]), AF.Copy, CT + ["aw_0"], ["cg"])
+    act(T.e15x[:], T.e15[:], AF.Copy, ["e15"], ["e15x"], scale=32.0)
+    act(T.e15n[:], T.e15[:], AF.Copy, ["e15"], ["e15n"], scale=-1.0)
+    act(T.e0x[:], T.e0[:], AF.Copy, ["e0"], ["e0x"], scale=16384.0)
+    pool(lambda p: p.affine_select(T.ea[:], T.e0x[:], GP, OP.not_equal, -16384.0, -1, 1), ["e0x"], ["ea"])
+    act(T.eb[:], T.e0[:], AF.Copy, ["e0"], ["eb"], scale=32.0)
+    act(T.g8[:], T.g1[:], AF.Copy, ["g1"], ["g8"], scale=8192.0)
+    act(T.gb[:], T.g1[:], AF.Copy, ["g1", "gb"], ["g8n"], scale=-8192.0)
+    ts(T.pm[:], T.pm0[:], 15, AND, ["pm0"], ["pm"])
+    tt(T.li[:], T.pm[:], T.c16[:], ADD, ["pm", "c16"], ["li"])
+    do("V", lambda v: v.tensor_tensor_scan(T.rv[:], T.half[:, 0:16], T.half[:, 16:32], 65536.0, MUL, ADD), ["half"], ["rv"])
+    tt(T.rv2[:], T.rv[:], T.mask[:, 0:16], ADD, ["rv", "mask"], ["rv2"])
+    scan(T.rv3[:], T.rsw[:, 0:16], T.rv2[:], MIN, MAX, ["rsw", "rv2"], ["rv3"])
+    wc = T.rv3[:, 15:16]
+    act(T.gw[:], T.g1[:], AF.Copy, ["g1", "rv3"], ["gw"], scale=wc)
+    for c in range(10):
+        act(T.gwa[:, 128 * c:128 * c + 128], T.gw[:], AF.Copy, ["gw"], ["gw%d" % c], scale=2.0 ** (24 - 16 * c))
+
+    def late_fills():
+        for c in range(10):
+            act(T.thr[:, c:c + 1], wc, AF.Copy, ["rv3"], ["thr"], scale=2.5 * 2.0 ** (24 - 16 * c))
+        act(T.li16[:], T.li[:], AF.Identity, ["li"], ["li16"], bias=OFF + 17.0, scale=16.0)
+        act(T.dum[:], T.li[:], AF.Identity, ["li"], ["dum"], bias=W + OFD, scale=1.0)
+        fill(T.acol[:], 1, 0.0, "acol")
+        fill(T.am[:, 0:1], 1, 0.0, "am0")
+        for j, v in enumerate(AC):
+            fill(T.ac[:, j:j + 1], 1, v, "ac%d" % j)
+        act(T.ta4[:], T.li16[:], AF.Identity, ["li16"], ["ta4"], bias=0.0, scale=1.0)
+        fill(T.ft[:], 32, 0.0, "ft")
+        fill(T.one5[:], 128, 512.0, "one5")
+        fill(T.wy[:, W:W + B], B, 0.0, "wyd")
+    for j in range(1, 4):
+        act(T.rs1[:, 224 * j:224 * j + 224], T.rs1[:, 0:224], AF.Copy, ["rs1_0"], ["rs1_%d" % j])
+    RS1 = ["rs1_%d" % j for j in range(4)]
+
+    WY = ["wy%d" % u for u in range(8)] + ["wyd"]
+    IL = ["il0", "il1"]
+
+    def unit(u):
+        c = u * UN
+        ts(T.tmp[:, c:c + UN], T.ilt[:, c:c + UN], 31, AND, ["il%d" % (u // 4)], ["tmp%d" % u])
+        cp(T.wy[:, c:c + UN], T.tmp[:, c:c + UN], ["tmp%d" % u], ["wy%d" % u])
+
+    for u in range(4):
+        unit(u)
+
+    def rewrite_prep(t):
+        d = T["r1_%d" % (t - 1)][:, 0:10]
+        cp(T.wold[:], T.wy[:].indirect(d), WY + ["r1_%d" % (t - 1)], ["wold"])
+        mm(T.b2[:, 0:B], T.i1[:], T.wold[:], True, True, ["i1", "wold"], ["b2"])
+
+    def rewrite(t):
+        tz = "rz_%d" % (t - 1)
+        d = T["r1_%d" % (t - 1)][:, 0:10]
+        tt(T.ui[:], T.b2[:, 0:B], T[tz][:], ADD, ["b2", tz], ["ui"])
+        ts(T.ui2[:], T.ui[:], 31, AND, ["ui"], ["ui2"])
+        cp(T.wy[:].indirect(d), T.ui2[:], ["ui2", "r1_%d" % (t - 1)], WY)
+
+    b = [T["b%d" % j] for j in range(8)]
+    P = lambda j: b[j][:, 0:B]
+    for t in range(RO):
+        last = t == RO - 1
+        m1, zs, m3 = T["m1_%d" % t], T["zs_%d" % t], T["m3_%d" % t]
+        if t == 0:
+            y, ty, aw, taw = T.y0t[:], "y0", T.aw0[:], "aw_0"
+            tfin, ttf = T.tf0[:], "tf0"
+        else:
+            y, ty = T["rz_%d" % (t - 1)][:], "rz_%d" % (t - 1)
+            aw, taw = T["r3_%d" % (t - 1)][:, 0:10], "r3_%d" % (t - 1)
+            tfin, ttf = T["r1_%d" % t][:, 10:20], "r1_%d" % t
+        for k, s in (("r1", "a1"), ("rz", "az"), ("r3", "a3")):
+            arrives("%s_%d" % (k, t), "%s_%d" % (s, t))
+        for j in (3, 4, 5, 7):
+            mm(P(j), T.i1[:], T.mask[:], True, False, ["i1", "mask"], ["b%d" % j])
+        if t > 0:
+            rewrite(t)
+        ts(T.y2[:], y, 2.0, MUL, [ty], ["y2"], 0.5, MAX)
+        if t > 0:
+            act(T.cg[:], T.colt[:].indirect(aw), AF.Copy, CT + [taw], ["cg"])
+        if t == 0:
+            ts(T.wgi[:], T.ilt[:].indirect(aw), 31, AND, IL + [taw], ["wgi"])
+            ts(T.lg[:], T.ilt[:].indirect(aw), 0.03125, MUL, IL + [taw], ["lg"], 136.0 - 31.0 / 64.0, ADD)
+            tt(T.wg[:], T.wgi[:], T.cg[:], ADD, ["wgi", "cg"], ["wg"])
+        else:
+            ts(T.lg[:], T.ilt[:].indirect(aw), 0.03125, MUL, IL + [taw], ["lg"], 136.0 - 31.0 / 64.0, ADD)
+            tt(T.wg[:], T.wy[:].indirect(aw), T.cg[:], ADD, WY + [taw, "cg"], ["wg"])
+        ts(T.sg[:], T.wg[:], 15.5, GE, ["wg"], ["sg"], 32.0, MUL)
+        if t > 0:
+            cp(T.xt[:, 0:16 * B].indirect(T["r3_%d" % (t - 1)][:, 10:20]), y, [ty, taw], ["x"])
+        else:
+            late_fills()
+
+        def part(j, what, first, stop):
+            lhs = {"l": ("i32", "e15x"), "w": ("i1", "e15"), "s": ("in1", "e15n")}[what][j > 1]
+            k = what + "g"
+            mm(P(j), T[lhs][:], T[k][:], first, stop, [lhs, k], ["b%d" % j])
+        part(1, "l", True, False)
+        part(2, "l", True, False)
+        part(1, "w", False, False)
+        part(2, "w", False, False)
+        part(1, "s", False, True)
+        part(2, "s", False, True)
+        part(3, "l", False, False)
+        part(3, "w", False, False)
+        part(3, "s", False, True)
+        ts(T.st[:], P(1), -OFD, ADD, ["b1"], ["st"])
+        for j, (lo, hi) in enumerate(SCH):
+            act(T.vv[:, 16 * lo:16 * hi], T.xt[:].indirect(T.st[:, lo:hi]), AF.Copy, ["x", "st"], ["vv%d" % j])
+        cp(T.dru[:], P(2), ["b2"], ["dru"])
+        if t > 0:
+            late[1](m1[:, 10:20], "m1t_%d" % t)
+        ts(T["awm%d" % (t % 2)][:], aw, -16.0 - 4096.0 - 131072.0, ADD, [taw], ["awm%d" % (t % 2)])
+        scan(T.dws[:], T.rsw[:], P(3), MIN, MAX, ["rsw", "b3"], ["dws"])
+        for c in range(10):
+            nn = B - 16 * c
+            e0 = c * B
+            ts(T.eq[:, e0:e0 + nn], T.dru[:, 16 * c:B], T.dws[:, 16 * c + 15:16 * c + 16], EQ, ["dru", "dws"], ["eq%d" % c])
+            mm(b[5][:, 16 * c:B], T.gwa[:, 128 * c:128 * c + 128], T.eq[:, e0:e0 + nn], False, c == 9, ["gw%d" % c, "eq%d" % c], ["b5"])
+        mm(b[0][:, 256:256 + B], T.i1[:], T.y2[:], True, True, ["i1", "y2"], ["b0"])
+        mm(b[6][:, 256:256 + B], T.in1[:], y, True, False, ["in1", ty], ["b6"])
+        mm(P(4), T.ea[:], T.lg[:], False, False, ["ea", "lg"], ["b4"])
+        mm(P(4), T.eb[:], T.lg[:], False, True, ["eb", "lg"], ["b4"])
+        mm(P(7), T.i1[:], T.cg[:], False, False, ["i1", "cg"], ["b7"])
+
+        def min4(j):
+            lo, hi = SCH[j]
+            scan(T.mn[:, 16 * lo:16 * hi], T.rs1[:, 0:16 * (hi - lo)], T.vv[:, 16 * lo:16 * hi], MAX, MIN, RS1 + ["vv%d" % j], ["mn%d" % j])
+
+        def max4(j):
+            lo, hi = SCH[j]
+            scan(T.mx[:, 4 * lo:4 * hi], T.rs2[:, 0:4 * (hi - lo)], T.mn[:, 16 * lo + 3:16 * hi:4], MIN, MAX, ["rs2", "mn%d" % j], ["mx%d" % j])
+        if t:
+            min4(0)
+        else:
+            unit(4)
+        scan(T.rs[:], T.rsw[:], P(5), MIN, MAX, ["rsw", "b5"], ["rs"])
+        if t:
+            max4(0)
+        tt(T.lose[:], T.rs[:, 15:B:16], T.thr[:], GE, ["rs", "thr"], ["lose"])
+        if t:
+            min4(1)
+        tt(T.lose2[:], T.lose[:], T.dum[:], MUL, ["lose", "dum"], ["lose2"])
+        if t:
+            max4(1)
+        tt(T.dd[:], T.lose2[:], T.dws[:, 15:B:16], MAX, ["lose2", "dws"], ["dd"])
+        if t:
+            min4(2)
+        ts(m1[:, 0:10], T.dd[:], -OFD, ADD, ["dd"], ["m1d_%d" % t])
+        wid = 10 if t == 0 else 20
+        send(T["r1_%d" % t][:, 0:wid], m1[:, 0:wid], ["m1d_%d" % t] + (["m1t_%d" % t] if t else []), "a1_%d" % t)
+        if t == 0:
+            unit(5)
+            unit(6)
+            min4(0)
+            min4(1)
+            max4(0)
+            max4(1)
+            min4(2)
+        max4(2)
+        min4(3)
+        max4(3)
+        mall = T.mx[:, 3:4 * B:4]
+        mtok = ["mx0", "mx1", "mx2", "mx3"]
+        mm(b[6][:, 256:256 + B], T.i1[:], T.mx[:, 3:4 * B:4], False, True, ["i1", "mx0", "mx1", "mx2", "mx3"], ["b6"])
+        act(T.kk2[:], mall, AF.Sign, mtok, ["kk2"])
+        act(zs[:], b[6][:, 256:256 + B], AF.Abs, ["b6"], ["zs_%d" % t])
+        send(T["rz_%d" % t][:], zs[:], ["zs_%d" % t], "az_%d" % t)
+        tt(T.kk[:], mall, b[0][:, 256:256 + B], GE, mtok + ["b0"], ["kk"])
+        scan(T.ps[:], T.rsw[:], P(4), MIN, MAX, ["rsw", "b4"], ["ps"])
+        ts(T.d0[:, 1:60:6], T.ps[:, 15:B:16], M16K, ADD, ["ps"], ["d0s"], M16K, SUB)
+        tt(T.d1[:, 1:60:6], T.d0[:, 1:60:6], T.ps[:, 15:B:16], SUB, ["d0s", "ps"], ["d1s"])
+        mm(P(7), T.gb[:], T.kk2[:], False, False, ["g8n", "kk2"], ["b7"])
+        mm(P(7), T.g8[:], T.kk[:], False, False, ["g8", "kk"], ["b7"])
+        mm(P(7), T.g1[:], zs[:], False, True, ["g1", "zs_%d" % t], ["b7"])
+        scan(T.qs[:], T.rsw[:], P(7), MIN, MAX, ["rsw", "b7"], ["qs"])
+        q = T.qs[:, 15:B:16]
+        act(T.d1[:, 2:60:6], q, AF.Identity, ["qs", "ac0"], ["d1x1"], bias=T.ac[:, 0:1])
+        act(T.d1[:, 5:60:6], q, AF.Identity, ["qs", "ac1"], ["d1x2"], bias=T.ac[:, 1:2])
+        if not last:
+            act(T.d1[:, 62:120:6], q, AF.Identity, ["qs", "ac2"], ["d1x3"], bias=T.ac[:, 2:3])
+        ts(T.d1[:, 0:60:6], q, 73711.5 - 131072.0, GE, ["qs"], ["d1b"], 1.0 / 512.0, MUL)
+
+        h = t % 2
+        am, awm, tam, tawm = T.am[:, h:h + 1], T["awm%d" % h][:], "am%d" % h, "awm%d" % h
+
+        def clock1(q=q, am=am, awm=awm, tam=tam, tawm=tawm, tfin=tfin, ttf=ttf):
+            tt(T.qi[:], q, awm, SUB, ["qs", tawm], ["qi"])
+            ts(T.tfa[:], tfin, am, ADD, [ttf, tam], ["tfa"], 1.0, ADD)
+            ts(T.qi2[:], T.qi[:], 31, AND, ["qi"], ["qi2"])
+
+        def clock2(out, tok):
+            tt(T.tfn[:], T.tfa[:], T.qi2[:], ADD, ["tfa", "qi2"], ["tfn"])
+            cp(out, T.tfn[:], ["tfn"], [tok])
+        toks = ["d0c", "d0s", "d1c", "d1s", "d1b", "d1x1", "d1x2"]
+        if last:
+            scan(T.po[:, 0:60], T.d0[:, 0:60], T.d1[:, 0:60], MUL, ADD, toks, ["po"])
+            ts(m3[:, 0:10], T.po[:, 5:60:6], -OFF, ADD, ["po"], ["m3a"])
+            clock1()
+            clock2(m3[:, 10:20], "m3b")
+            send(T["r3_%d" % t][:], m3[:], ["m3a", "m3b"], "a3_%d" % t)
+        else:
+            tt(T.d1[:, 65:120:6], q, T.ta4[:], ADD, ["qs", "ta4"], ["d1x4"])
+            scan(T.po[:], T.d0[:], T.d1[:], MUL, ADD, toks + ["d1x3", "d1x4"], ["po"])
+            ts(m3[:], T.po[:, 5:120:6], -OFF, ADD, ["po"], ["m3_%d" % t])
+            send(T["r3_%d" % t][:], m3[:], ["m3_%d" % t], "a3_%d" % t)
+            mm(b[0][:, 0:10], T.one5[:], T.d1[:, 0:60:6], True, True, ["one5", "d1b"], ["b0"])
+            if t == 0:
+                unit(7)
+            do("V", lambda v: v.tensor_reduce(T.acol[:], b[0][:, 0:10], AxisListType.X, ADD), ["b0"], ["acol"])
+            for j, v in enumerate(AC):
+                act(T.ac[:, j:j + 1], T.acol[:], AF.Identity, ["acol"], ["ac%d" % j], bias=v, scale=1.0)
+            act(T.ta4[:], T.li16[:], AF.Identity, ["li16", "acol"], ["ta4"], bias=T.acol[:], scale=1.0)
+            act(T.am1[:], T.acol[:], AF.Identity, ["acol"], ["am1"], bias=-15.5, scale=1.0)
+            act(T.am2[:], T.am1[:], AF.Identity, ["am1"], ["am2"], bias=M32, scale=1.0)
+            act(T.am3[:], T.am2[:], AF.Identity, ["am2"], ["am3"], bias=-M32, scale=1.0)
+            act(T.am[:, 1 - h:2 - h], T.am3[:], AF.Identity, ["am3", "acol"], ["am%d" % (1 - h)], bias=T.acol[:], scale=-1.0)
+        late = (clock1, clock2)
+        rewrite_prep(t + 1)
+        if not last:
+            clock1()
+    rewrite(RO)
+    dma("Y", T.yw[:], T.wy[:, 0:W], WY, [], "oyw")
+    dma("S", T.yy[:], T["rz_3"][:], ["rz_3"], [], "oyy")
+    cp(T.fi[:], T["r3_3"][:], ["r3_3"], ["fi"])
+    ts(T.fi2[:, 0:10], T.fi[:, 0:10], 5, SHR, ["fi"], ["fi2a"])
+    ts(T.fi2[:, 10:20], T.fi[:, 10:20], 4095, AND, ["fi"], ["fi2b"])
+    cp(T.ft[:, 0:20], T.fi2[:], ["fi2a", "fi2b"], ["ft"])
+    do("V", lambda v: v.transpose(T.ftt[:], T.ft[:]), ["ft"], ["ftt"])
+    for a in range(4):
+        for h in range(2):
+            r = 2 * a + h
+            dma("S", T.yl[r:r + 1, :], T.ftt[32 * a:32 * a + 10, 16 * h:16 * h + 16], ["ftt"], [], "osm")
+            dma("Y", T.yt[r:r + 1, :], T.ftt[32 * a + 10:32 * a + 20, 16 * h:16 * h + 16], ["ftt"], [], "osn")
+    g.wait_ge(T.sem.loc, sent[0])
+    for s, v in tot.items():
+        if know["P"].get(s, 0) < v:
+            g.wait_ge(T.sem[s], v)

@@ -1,61 +1,47 @@
-from concourse.mybir import AluOpType, AxisListType, ActivationFunctionType
+from concourse.mybir import AluOpType, ActivationFunctionType
 
 W, B, RO = 3712, 160, 4
-UN = 464
-SCH = [(0, 56), (56, 112), (112, 144), (144, 160)]
+PIECES = [(0, 2208), (2208, W)]
+UNITS = [(0, 736), (736, 1472), (1472, 2208), (2208, 2712), (2712, 3216), (3216, W)]
+VCH = (0, 40)
+SCH = [(40, 88), (88, 128), (128, 152), (152, 160)]
 OFF = 4352.0
-OFD = OFF - 16.0
+OFD = OFF + 16.0
+NS = 4
 M32 = 402653184.0
 M16 = 201326592.0
 M16K = 1.5 * 2.0 ** 37
-AC = (17.0 - 15.5, 17.0, 17.0 - 7.5)
 
-SCRATCH = {
-    "ilt": ("sbuf", [128, W], "int32"), "tmp": ("sbuf", [128, W], "int32"),
-    "xt": ("sbuf", [128, W], "bfloat16"), "wy": ("sbuf", [128, W + B], "bfloat16"),
-    "colt": ("sbuf", [128, W], "bfloat16"),
-    "vv": ("sbuf", [128, 16 * B], "bfloat16"), "mn": ("sbuf", [128, 16 * B], "bfloat16"), "mx": ("sbuf", [128, 4 * B], "bfloat16"),
-    "eq": ("sbuf", [128, 10 * B], "bfloat16"), "dru": ("sbuf", [128, B], "uint16"),
-    "y0t": ("sbuf", [128, B], "bfloat16"),
-    "ln8": ("sbuf", [8, B], "int32"), "tk8": ("sbuf", [8, B], "int32"), "ti8": ("sbuf", [8, B], "int32"), "th8": ("sbuf", [8, B], "int32"),
-    "lb8": ("sbuf", [8, B], "bfloat16"), "tb8": ("sbuf", [8, B], "bfloat16"), "tc8": ("sbuf", [8, B], "bfloat16"),
-    "sel": ("sbuf", [8, 128], "bfloat16"), "sel32": ("sbuf", [8, 128], "bfloat16"), "tf0": ("sbuf", [128, 10], "float32"),
-    "ac": ("sbuf", [128, 3], "float32"), "awm0": ("sbuf", [128, 10], "float32"), "awm1": ("sbuf", [128, 10], "float32"), "thr": ("sbuf", [128, 10], "float32"),
-    "wg": ("sbuf", [128, B], "bfloat16"), "wgi": ("sbuf", [128, B], "int32"), "lg": ("sbuf", [128, B], "bfloat16"), "cg": ("sbuf", [128, B], "bfloat16"), "sg": ("sbuf", [128, B], "bfloat16"),
-    "st": ("sbuf", [128, B], "uint16"), "kk": ("sbuf", [128, B], "bfloat16"),
-    "ui": ("sbuf", [128, B], "int32"), "ui2": ("sbuf", [128, B], "int32"), "wold": ("sbuf", [128, B], "bfloat16"),
-    "dws": ("sbuf", [128, B], "float32"), "ps": ("sbuf", [128, B], "float32"), "rs": ("sbuf", [128, B], "float32"), "qs": ("sbuf", [128, B], "float32"),
-    "lose": ("sbuf", [128, 10], "float32"), "lose2": ("sbuf", [128, 10], "float32"), "dd": ("sbuf", [128, 10], "float32"),
-    "d0": ("sbuf", [128, 120], "float32"), "d1": ("sbuf", [128, 120], "float32"), "po": ("sbuf", [128, 120], "float32"),
-    "ta4": ("sbuf", [128, 10], "float32"),
-    "acol": ("sbuf", [128, 1], "float32"), "am1": ("sbuf", [128, 1], "float32"), "am2": ("sbuf", [128, 1], "float32"), "am3": ("sbuf", [128, 1], "float32"), "am": ("sbuf", [128, 2], "float32"),
-    "tfa": ("sbuf", [128, 10], "float32"), "qi": ("sbuf", [128, 10], "int32"), "qi2": ("sbuf", [128, 10], "int32"), "tfn": ("sbuf", [128, 10], "float32"),
-    "aw0": ("sbuf", [128, 10], "uint16"),
-    "fi": ("sbuf", [128, 20], "int32"), "fi2": ("sbuf", [128, 20], "int32"), "ft": ("sbuf", [128, 32], "float32"), "ftt": ("sbuf", [128, 32], "float32"),
-    "ones": ("sbuf", [128, 224], "bfloat16"), "g1": ("sbuf", [128, 128], "bfloat16"), "gb": ("sbuf", [128, 128], "bfloat16"), "i1": ("sbuf", [128, 128], "bfloat16"),
-    "i32": ("sbuf", [128, 128], "bfloat16"), "in1": ("sbuf", [128, 128], "bfloat16"),
-    "g8": ("sbuf", [128, 128], "bfloat16"), "gw": ("sbuf", [128, 128], "bfloat16"),
-    "e15": ("sbuf", [128, 128], "bfloat16"), "e15x": ("sbuf", [128, 128], "bfloat16"), "e15n": ("sbuf", [128, 128], "bfloat16"),
-    "ea": ("sbuf", [128, 128], "bfloat16"), "eb": ("sbuf", [128, 128], "bfloat16"), "one5": ("sbuf", [128, 128], "float32"),
-    "pq": ("sbuf", [128, B], "int32"), "pq2": ("sbuf", [128, B], "int32"), "mask": ("sbuf", [128, B], "bfloat16"), "q16": ("sbuf", [128, B], "float32"), "rsw": ("sbuf", [128, B], "float32"),
-    "rs1": ("sbuf", [128, 896], "bfloat16"), "rs2": ("sbuf", [128, 224], "bfloat16"),
-    "pm0": ("sbuf", [128, 10], "int32"), "pm": ("sbuf", [128, 10], "int32"), "c16": ("sbuf", [128, 10], "int32"),
-    "li": ("sbuf", [128, 10], "float32"), "li16": ("sbuf", [128, 10], "float32"), "dum": ("sbuf", [128, 10], "float32"),
-    "gwa": ("sbuf", [128, 1280], "bfloat16"), "e0": ("sbuf", [128, 128], "bfloat16"), "e0x": ("sbuf", [128, 128], "bfloat16"),
-    "half": ("sbuf", [128, 32], "float32"), "rv": ("sbuf", [128, 16], "float32"), "rv2": ("sbuf", [128, 16], "float32"), "rv3": ("sbuf", [128, 16], "float32"),
-    "y2": ("sbuf", [128, B], "bfloat16"), "kk2": ("sbuf", [128, B], "bfloat16"),
-}
+F32, BF, I32, U16 = "float32", "bfloat16", "int32", "uint16"
+SCRATCH = {}
+for _dt, _rows, _list in (
+    (I32, 128, {"ilt": W, "tmp": W, "wgi": B, "ui": B, "ui2": B, "pq": B, "pq2": B, "pm0": 10, "pm": 10, "c16": 10,
+                "fa": 80, "fb": 80, "fc": 40, "fd": 20, "fe": 10, "ff": 10, "fg": 10}),
+    (BF, 128, {"xt": W, "wy": W + B, "colt": W, "vv": 16 * B, "mn": 16 * B, "mx": 4 * B, "eq": 10 * B, "y0t": B, "cg": B, "kk": B, "kk2": B,
+               "ones": 224, "g1": 128, "gb": 128, "i1": 128, "i32": 128, "in1": 128, "g8": 128, "e15": 128, "e15x": 128, "e15n": 128,
+               "ea": 128, "eb": 128, "e0": 128, "e0x": 128, "mask": B, "ab": 4 * B, "es": 4 * B, "in16": 128, "e15m": 128, "rs1": 768, "rs2": 224}),
+    (F32, 128, {"dws": B, "ps": B, "rs": B, "qs": B, "q16": B, "rsw": B, "dumr": B, "d0": 120, "d1": 120, "po": 120, "t1": 10, "li": 10,
+                "am": 4, "junk": 10, "onef": 128, "idf": 128, "hb": 120}),
+    (U16, 128, {"st": B, "aw0": 10, "raw": 10, "dst": 10}),
+    (I32, 8, {"ln8": B, "tk8": B, "ti8": B, "th8": B}),
+    (BF, 8, {"lb8": B, "tb8": B, "tc8": B, "sel": 128, "sel32": 128}),
+    (F32, 8, {"fin": 2 * B}),
+):
+    for _k, _n in _list.items():
+        SCRATCH[_k] = ("sbuf", [_rows, _n], _dt)
 for _t in range(RO):
-    SCRATCH["m1_%d" % _t] = ("sbuf", [128, 20], "uint16")
-    SCRATCH["zs_%d" % _t] = ("sbuf", [128, B], "bfloat16")
-    SCRATCH["m3_%d" % _t] = ("sbuf", [128, 20], "uint16")
-    SCRATCH["r1_%d" % _t] = ("sbuf", [128, 20], "uint16")
-    SCRATCH["rz_%d" % _t] = ("sbuf", [128, B], "bfloat16")
-    SCRATCH["r3_%d" % _t] = ("sbuf", [128, 20], "uint16")
+    for _k in ("op", "ro"):
+        SCRATCH["%s_%d" % (_k, _t)] = ("sbuf", [128, 3 * B], BF)
+    for _k in ("zs", "rz"):
+        SCRATCH["%s_%d" % (_k, _t)] = ("sbuf", [128, B], BF)
+    for _k in ("m3", "r3"):
+        SCRATCH["%s_%d" % (_k, _t)] = ("sbuf", [128, 20], U16)
+for _t in range(RO + 1):
+    SCRATCH["hs_%d" % _t] = ("sbuf", [128, 30], F32)
 for _t in range(8):
-    SCRATCH["b%d" % _t] = ("psum", [128, 512], "float32")
+    SCRATCH["b%d" % _t] = ("psum", [128, 512], F32)
 SEMAPHORES = ["qV", "qS", "qT", "qP", "loc", "dil0", "dil1", "dx", "dy", "dln", "dtk", "oyy", "oyw", "osm", "osn"]
-SEMAPHORES += ["a%s_%d" % (m, t) for m in ("1", "z", "3") for t in range(RO)]
+SEMAPHORES += ["a%s_%d" % (m, t) for m in ("o", "z", "3") for t in range(RO)] + ["ah_%d" % t for t in range(RO + 1)]
 
 
 def rank_program(g, core, T, topo):
@@ -63,7 +49,6 @@ def rank_program(g, core, T, topo):
     if rank is None:
         return
     n = len(T.cores)
-    nxt, prv = T.cores[(rank + 1) % n], T.cores[(rank - 1) % n]
     OP, AF = AluOpType, ActivationFunctionType
     ADD, SUB, MUL, MAX, MIN, EQ, GE, GT = OP.add, OP.subtract, OP.mult, OP.max, OP.min, OP.is_equal, OP.is_ge, OP.is_gt
     AND, SHR = OP.bitwise_and, OP.arith_shift_right
@@ -121,76 +106,68 @@ def rank_program(g, core, T, topo):
     def cp(out, a, r, w):
         do("V", lambda v: v.tensor_copy(out, a), r, w)
 
-    def ms(ap, val, w):
-        do("V", lambda v: v.memset(ap, val), [], w)
-
     def scan(out, x0, x1, o0, o1, r, w):
         do("V", lambda v: v.tensor_tensor_scan(out, x0, x1, 0.0, o0, o1), r, w)
 
     def mm(out, lhs, rhs, start, stop, r, w):
         do("T", lambda v: v.matmul(out, lhs, rhs, start, stop), r, w)
 
-    def act(out, in_, func, r, w, bias=None, scale=None):
-        if scale is not None and bias is not None:
-            do("S", lambda v: v.activation(out, in_, func, bias=bias, scale=scale), r, w)
-        elif scale is not None:
-            do("S", lambda v: v.activation(out, in_, func, scale=scale), r, w)
-        elif bias is None:
-            do("S", lambda v: v.activation(out, in_, func), r, w)
-        else:
-            do("S", lambda v: v.activation(out, in_, func, bias=bias), r, w)
-
-    sent = [0]
-    rid, pid, _se = topo.addr(nxt)
-    msk, ne = topo.mask(core, nxt), len(topo.engines(core, nxt))
-    na = len(topo.engines(prv, core))
-
-    def send(out, in_, r, sem):
-        waits("P", r, [])
-        g.remote_dma(out, in_, T.sem[sem], T.sem.loc, pid, rid, msk)
-        sent[0] += ne
-
-    def arrives(tok, sem):
-        lastw[tok] = [(sem, na, {sem: na})]
-        tot[sem] = na
-
-    dma("Y", T.ln8[:], T.ln0[:], [], ["ln8"], "dln")
-    dma("Y", T.tk8[:], T.tk0[:], [], ["tk8"], "dtk")
-    for q in range(2):
-        c = q * 1856
-        dma("Y", T.ilt[:, c:c + 1856], T.il[:, c:c + 1856], [], ["il%d" % q], "dil%d" % q)
-    dma("Y", T.xt[:], T.xw[:], [], ["x"], "dx")
-    dma("S", T.y0t[:], T.y0[:], [], ["y0"], "dy")
+    def act(out, in_, func, r, w, **kw):
+        do("S", lambda v: v.activation(out, in_, func, **kw), r, w)
 
     def pool(fn, r, w):
         do("P", fn, r, w)
-    ms(T.ones[:], 1.0, ["ones"])
+
+    sent = [0]
+
+    def send(hops, out, in_, r, sem):
+        waits("P", r, [])
+        to = T.cores[(rank + hops) % n]
+        rid, pid, _se = topo.addr(to)
+        g.remote_dma(out, in_, T.sem[sem], T.sem.loc, pid, rid, topo.mask(core, to))
+        sent[0] += len(topo.engines(core, to))
+
+    def arrives(hops, tok, sem):
+        na = len(topo.engines(T.cores[(rank - hops) % n], core))
+        lastw[tok] = [(sem, na, {sem: na})]
+        tot[sem] = na
+
+    b = [T["b%d" % j] for j in range(8)]
+    P = lambda j: b[j][:, 0:B]
+
+    dma("Y", T.ln8[:], T.ln0[:], [], ["ln8"], "dln")
+    dma("S", T.tk8[:], T.tk0[:], [], ["tk8"], "dtk")
+    for q, (lo, hi) in enumerate(PIECES):
+        dma("Y", T.ilt[:, lo:hi], T.il[:, lo:hi], [], ["il%d" % q], "dil%d" % q)
+    dma("Y", T.xt[:], T.xw[:], [], ["x"], "dx")
+    dma("Y", T.y0t[:], T.y0[:], [], ["y0"], "dy")
+
+    do("V", lambda v: v.memset(T.ones[:], 1.0), [], ["ones"])
     pool(lambda p: p.iota(T.pq[:], [[0, 10], [1, 16]], 128, -1), [], ["pq"])
     pool(lambda p: p.iota(T.q16[:], [[0, 10], [1, 16]], 0, 0, allow_small_or_imprecise_dtypes=True), [], ["q16"])
     pool(lambda p: p.affine_select(T.i1[:], T.ones[:, 0:128], [[-1, 128]], EQ, 0.0, 0, 1), ["ones"], ["i1"])
     pool(lambda p: p.affine_select(T.sel[:], T.ones[0:8, 0:128], [[1, 8], [0, 16]], EQ, 0.0, 0, -1), ["ones"], ["sel"])
     pool(lambda p: p.iota(T.pm0[:], [[0, 10]], 0, 1), [], ["pm0"])
     pool(lambda p: p.iota(T.c16[:], [[16, 10]], 0, 0), [], ["c16"])
-    pool(lambda p: p.iota(T.colt[:, 0:928], [[0, 29], [1, 32]], -16, 0, allow_small_or_imprecise_dtypes=True), [], ["colt0"])
+    pool(lambda p: p.iota(T.colt[:, 0:928], [[0, 29], [1, 32]], 0, 0, allow_small_or_imprecise_dtypes=True), [], ["colt0"])
     pool(lambda p: p.affine_select(T.gb[:], T.ones[:, 0:128], [[-16, 8], [0, 16]], GE, 0.0, 0, 1), ["ones"], ["gb"])
     pool(lambda p: p.affine_select(T.g1[:], T.gb[:], [[16, 8], [0, 16]], GE, 0.0, 15, -1), ["gb"], ["g1"])
 
     def fill(ap, n_, v, w):
         act(ap, T.ones[:, 0:n_], AF.Copy, ["ones"], [w], scale=v)
-    fill(T.half[:, 0:16], 16, 0.5, "half")
-    fill(T.half[:, 16:32], 16, 0.0, "half")
     fill(T.d0[:], 120, 1.0, "d0c")
-    for lo, hi, v in ((0, 60, 0.0), (5, 60, -1.0), (60, 120, 0.0), (61, 120, 0.0), (62, 120, 0.0), (65, 120, -1.0)):
-        fill(T.d0[:, lo:hi:6], 10, v, "d0c")
+    for lo, v in ((0, 0.0), (5, -1.0)):
+        fill(T.d0[:, lo:120:6], 20, v, "d0c")
     fill(T.d1[:], 120, 0.0, "d1c")
     for lo, hi, v in ((3, 60, M32), (4, 60, -M32), (63, 120, M16), (64, 120, -M16)):
         fill(T.d1[:, lo:hi:6], 10, v, "d1c")
-    for k in ("d1b", "d1s", "d1x1", "d1x2", "d1x3", "d1x4"):
+    for k in ("d1b", "d1s", "d1x0", "d1x1", "d1x2", "d1x3"):
         lastw[k] = lastw["d1c"]
     lastw["d0s"] = lastw["d0c"]
     fill(T.rs2[:], 224, 0.0, "rs2")
+    fill(T.dumr[:], B, 0.0, "dumr")
     Q4 = [[0, 56], [1, 4]]
-    pool(lambda p: p.affine_select(T.rs1[:, 0:224], T.rs2[:], Q4, OP.not_equal, 512.0, 0, 0), ["rs2"], ["rs1_0"])
+    pool(lambda p: p.affine_select(T.rs1[:, 0:192], T.rs2[:, 0:192], [[0, 48], [1, 4]], OP.not_equal, 512.0, 0, 0), ["rs2"], ["rs1_0"])
     pool(lambda p: p.affine_select(T.rs2[:], T.rs2[:], Q4, EQ, 512.0, 0, 0), ["rs2"], ["rs2"])
     CT = ["colt%d" % j for j in range(4)]
 
@@ -203,14 +180,15 @@ def rank_program(g, core, T, topo):
     ts(T.th8[:], T.tk8[:], 5, SHR, ["tk8"], ["th8"])
     cp(T.tb8[:], T.ti8[:], ["ti8"], ["tb8"])
     cp(T.tc8[:], T.th8[:], ["th8"], ["tc8"])
-    for bb, tb, hi, thi in ((T.b0, "b0", T.lb8, "lb8"), (T.b1, "b1", T.tc8, "tc8")):
-        mm(bb[:, 0:B], T.i1[:], T.mask[:], True, False, ["i1", "mask"], [tb])
-        mm(bb[:, 0:B], T.sel32[:], hi[:], False, False, ["sel32", thi], [tb])
-        mm(bb[:, 0:B], T.sel[:], T.tb8[:], False, True, ["sel", "tb8"], [tb])
-    scan(T.qs[:], T.rsw[:], T.b0[:, 0:B], MIN, MAX, ["rsw", "b0"], ["qs"])
+    for j, hi in ((0, "lb8"), (1, "tc8")):
+        mm(P(j), T.i1[:], T.mask[:], True, False, ["i1", "mask"], ["b%d" % j])
+        mm(P(j), T.sel32[:], T[hi][:], False, False, ["sel32", hi], ["b%d" % j])
+        mm(P(j), T.sel[:], T.tb8[:], False, True, ["sel", "tb8"], ["b%d" % j])
+    scan(T.qs[:], T.rsw[:], P(0), MIN, MAX, ["rsw", "b0"], ["qs"])
     cp(T.aw0[:], T.qs[:, 15:B:16], ["qs"], ["aw_0"])
-    scan(T.ps[:], T.rsw[:], T.b1[:, 0:B], MIN, MAX, ["rsw", "b1"], ["ps"])
-    cp(T.tf0[:], T.ps[:, 15:B:16], ["ps"], ["tf0"])
+    scan(T.ps[:], T.rsw[:], P(1), MIN, MAX, ["rsw", "b1"], ["ps"])
+    act(T.hs_0[:, 0:10], T.ps[:, 15:B:16], AF.Identity, ["ps"], ["hsa_0"], bias=float(RO))
+    act(T.hs_0[:, 10:20], T.ps[:, 15:B:16], AF.Copy, ["ps"], ["hsb_0"])
 
     GP = [[-16, 8], [0, 16]]
     pool(lambda p: p.affine_select(T.e15[:], T.ones[:, 0:128], GP, EQ, 0.0, -15, 1), ["ones"], ["e15"])
@@ -219,239 +197,204 @@ def rank_program(g, core, T, topo):
     act(T.in1[:], T.i1[:], AF.Copy, ["i1"], ["in1"], scale=-1.0)
     for j in range(1, 4):
         act(T.colt[:, 928 * j:928 * j + 928], T.colt[:, 0:928], AF.Copy, ["colt0"], ["colt%d" % j])
-    act(T.cg[:], T.colt[:].indirect(T.aw0[:]), AF.Copy, CT + ["aw_0"], ["cg"])
     act(T.e15x[:], T.e15[:], AF.Copy, ["e15"], ["e15x"], scale=32.0)
-    act(T.e15n[:], T.e15[:], AF.Copy, ["e15"], ["e15n"], scale=-1.0)
+    act(T.e15n[:], T.e15[:], AF.Copy, ["e15"], ["e15n"], scale=-16.0)
+    act(T.in16[:], T.i1[:], AF.Copy, ["i1"], ["in16"], scale=-16.0)
     act(T.e0x[:], T.e0[:], AF.Copy, ["e0"], ["e0x"], scale=16384.0)
     pool(lambda p: p.affine_select(T.ea[:], T.e0x[:], GP, OP.not_equal, -16384.0, -1, 1), ["e0x"], ["ea"])
+    send(RO, T.hb[:, 0:20], T.hs_0[:, 0:20], ["hsa_0", "hsb_0"], "ah_0")
     act(T.eb[:], T.e0[:], AF.Copy, ["e0"], ["eb"], scale=32.0)
     act(T.g8[:], T.g1[:], AF.Copy, ["g1"], ["g8"], scale=8192.0)
     act(T.gb[:], T.g1[:], AF.Copy, ["g1", "gb"], ["g8n"], scale=-8192.0)
     ts(T.pm[:], T.pm0[:], 15, AND, ["pm0"], ["pm"])
     tt(T.li[:], T.pm[:], T.c16[:], ADD, ["pm", "c16"], ["li"])
-    do("V", lambda v: v.tensor_tensor_scan(T.rv[:], T.half[:, 0:16], T.half[:, 16:32], 65536.0, MUL, ADD), ["half"], ["rv"])
-    tt(T.rv2[:], T.rv[:], T.mask[:, 0:16], ADD, ["rv", "mask"], ["rv2"])
-    scan(T.rv3[:], T.rsw[:, 0:16], T.rv2[:], MIN, MAX, ["rsw", "rv2"], ["rv3"])
-    wc = T.rv3[:, 15:16]
-    act(T.gw[:], T.g1[:], AF.Copy, ["g1", "rv3"], ["gw"], scale=wc)
-    for c in range(10):
-        act(T.gwa[:, 128 * c:128 * c + 128], T.gw[:], AF.Copy, ["gw"], ["gw%d" % c], scale=2.0 ** (24 - 16 * c))
-
-    def late_fills():
-        for c in range(10):
-            act(T.thr[:, c:c + 1], wc, AF.Copy, ["rv3"], ["thr"], scale=2.5 * 2.0 ** (24 - 16 * c))
-        act(T.li16[:], T.li[:], AF.Identity, ["li"], ["li16"], bias=OFF + 17.0, scale=16.0)
-        act(T.dum[:], T.li[:], AF.Identity, ["li"], ["dum"], bias=W + OFD, scale=1.0)
-        fill(T.acol[:], 1, 0.0, "acol")
-        fill(T.am[:, 0:1], 1, 0.0, "am0")
-        for j, v in enumerate(AC):
-            fill(T.ac[:, j:j + 1], 1, v, "ac%d" % j)
-        act(T.ta4[:], T.li16[:], AF.Identity, ["li16"], ["ta4"], bias=0.0, scale=1.0)
-        fill(T.ft[:], 32, 0.0, "ft")
-        fill(T.one5[:], 128, 512.0, "one5")
-        fill(T.wy[:, W:W + B], B, 0.0, "wyd")
+    act(T.d1[:, 60:120:6], T.li[:], AF.Identity, ["li"], ["d1c"], bias=-OFF - 6.5, scale=-16.0)
+    act(T.dumr[:, 0:B:16], T.li[:], AF.Identity, ["li"], ["dumr"], bias=W + OFD)
+    fill(T.am[:], 4, 0.0, "am0")
+    fill(T.onef[:], 128, 1.0, "onef")
+    act(T.idf[:], T.i1[:], AF.Copy, ["i1"], ["idf"])
+    fill(T.wy[:, W:W + B], B, 0.0, "wyd")
     for j in range(1, 4):
-        act(T.rs1[:, 224 * j:224 * j + 224], T.rs1[:, 0:224], AF.Copy, ["rs1_0"], ["rs1_%d" % j])
+        act(T.rs1[:, 192 * j:192 * j + 192], T.rs1[:, 0:192], AF.Copy, ["rs1_0"], ["rs1_%d" % j])
     RS1 = ["rs1_%d" % j for j in range(4)]
 
-    WY = ["wy%d" % u for u in range(8)] + ["wyd"]
+    WY = ["wy%d" % u for u in range(len(UNITS))] + ["wyd"]
     IL = ["il0", "il1"]
 
-    def unit(u):
-        c = u * UN
-        ts(T.tmp[:, c:c + UN], T.ilt[:, c:c + UN], 31, AND, ["il%d" % (u // 4)], ["tmp%d" % u])
-        cp(T.wy[:, c:c + UN], T.tmp[:, c:c + UN], ["tmp%d" % u], ["wy%d" % u])
+    def unit(u, on_pool=False):
+        lo, hi = UNITS[u]
+        ts(T.tmp[:, lo:hi], T.ilt[:, lo:hi], 31, AND, ["il%d" % (lo >= PIECES[1][0])], ["tmp%d" % u])
+        if on_pool:
+            pool(lambda p: p.affine_select(T.wy[:, lo:hi], T.tmp[:, lo:hi], [[0, hi - lo]], GE, 0.0, 0, 0), ["tmp%d" % u], ["wy%d" % u])
+        else:
+            cp(T.wy[:, lo:hi], T.tmp[:, lo:hi], ["tmp%d" % u], ["wy%d" % u])
 
-    for u in range(4):
+    for u in range(3):
         unit(u)
 
-    def rewrite_prep(t):
-        d = T["r1_%d" % (t - 1)][:, 0:10]
-        cp(T.wold[:], T.wy[:].indirect(d), WY + ["r1_%d" % (t - 1)], ["wold"])
-        mm(T.b2[:, 0:B], T.i1[:], T.wold[:], True, True, ["i1", "wold"], ["b2"])
+    def twice(y, ty):
+        act(P(0), y, AF.Relu, [ty], ["b0"], scale=2.0, bias=-1.0)
 
-    def rewrite(t):
-        tz = "rz_%d" % (t - 1)
-        d = T["r1_%d" % (t - 1)][:, 0:10]
-        tt(T.ui[:], T.b2[:, 0:B], T[tz][:], ADD, ["b2", tz], ["ui"])
-        ts(T.ui2[:], T.ui[:], 31, AND, ["ui"], ["ui2"])
-        cp(T.wy[:].indirect(d), T.ui2[:], ["ui2", "r1_%d" % (t - 1)], WY)
+    def min4(lo, hi):
+        scan(T.mn[:, 16 * lo:16 * hi], T.rs1[:, 0:16 * (hi - lo)], T.vv[:, 16 * lo:16 * hi], MAX, MIN, RS1 + ["vv%d" % lo], ["mn%d" % lo])
 
-    b = [T["b%d" % j] for j in range(8)]
-    P = lambda j: b[j][:, 0:B]
+    def max4(chunks):
+        lo, hi = chunks[0][0], chunks[-1][1]
+        scan(T.mx[:, 4 * lo:4 * hi], T.rs2[:, 0:4 * (hi - lo)], T.mn[:, 16 * lo + 3:16 * hi:4], MIN, MAX,
+             ["rs2"] + ["mn%d" % c[0] for c in chunks], ["mx%d" % lo])
+        return "mx%d" % lo
+
     for t in range(RO):
         last = t == RO - 1
-        m1, zs, m3 = T["m1_%d" % t], T["zs_%d" % t], T["m3_%d" % t]
+        op, zs, m3, ro, rz, hs = (T[k % t] for k in ("op_%d", "zs_%d", "m3_%d", "ro_%d", "rz_%d", "hs_%d"))
+        hs = T["hs_%d" % (t + 1)]
+        lg, wg, sg = op[:, 0:B], op[:, B:2 * B], op[:, 2 * B:3 * B]
         if t == 0:
             y, ty, aw, taw = T.y0t[:], "y0", T.aw0[:], "aw_0"
-            tfin, ttf = T.tf0[:], "tf0"
         else:
             y, ty = T["rz_%d" % (t - 1)][:], "rz_%d" % (t - 1)
             aw, taw = T["r3_%d" % (t - 1)][:, 0:10], "r3_%d" % (t - 1)
-            tfin, ttf = T["r1_%d" % t][:, 10:20], "r1_%d" % t
-        for k, s in (("r1", "a1"), ("rz", "az"), ("r3", "a3")):
-            arrives("%s_%d" % (k, t), "%s_%d" % (s, t))
-        for j in (3, 4, 5, 7):
-            mm(P(j), T.i1[:], T.mask[:], True, False, ["i1", "mask"], ["b%d" % j])
-        if t > 0:
-            rewrite(t)
-        ts(T.y2[:], y, 2.0, MUL, [ty], ["y2"], 0.5, MAX)
-        if t > 0:
-            act(T.cg[:], T.colt[:].indirect(aw), AF.Copy, CT + [taw], ["cg"])
+        arrives(1, "ro_%d" % t, "ao_%d" % t)
+        arrives(1, "rz_%d" % t, "az_%d" % t)
+        if not last:
+            arrives(1, "r3_%d" % t, "a3_%d" % t)
+        act(T.cg[:], T.colt[:].indirect(aw), AF.Copy, CT + [taw], ["cg"])
+        act(lg, T.ilt[:].indirect(aw), AF.Identity, IL + [taw], ["lg"], scale=0.03125, bias=136.0 - 31.0 / 64.0)
         if t == 0:
             ts(T.wgi[:], T.ilt[:].indirect(aw), 31, AND, IL + [taw], ["wgi"])
-            ts(T.lg[:], T.ilt[:].indirect(aw), 0.03125, MUL, IL + [taw], ["lg"], 136.0 - 31.0 / 64.0, ADD)
-            tt(T.wg[:], T.wgi[:], T.cg[:], ADD, ["wgi", "cg"], ["wg"])
+            tt(wg, T.wgi[:], T.cg[:], ADD, ["wgi", "cg"], ["wg"])
         else:
-            ts(T.lg[:], T.ilt[:].indirect(aw), 0.03125, MUL, IL + [taw], ["lg"], 136.0 - 31.0 / 64.0, ADD)
-            tt(T.wg[:], T.wy[:].indirect(aw), T.cg[:], ADD, WY + [taw, "cg"], ["wg"])
-        ts(T.sg[:], T.wg[:], 15.5, GE, ["wg"], ["sg"], 32.0, MUL)
-        if t > 0:
+            tt(wg, T.wy[:].indirect(aw), T.cg[:], ADD, WY + [taw, "cg"], ["wg"])
             cp(T.xt[:, 0:16 * B].indirect(T["r3_%d" % (t - 1)][:, 10:20]), y, [ty, taw], ["x"])
-        else:
-            late_fills()
-
-        def part(j, what, first, stop):
-            lhs = {"l": ("i32", "e15x"), "w": ("i1", "e15"), "s": ("in1", "e15n")}[what][j > 1]
-            k = what + "g"
-            mm(P(j), T[lhs][:], T[k][:], first, stop, [lhs, k], ["b%d" % j])
-        part(1, "l", True, False)
-        part(2, "l", True, False)
-        part(1, "w", False, False)
-        part(2, "w", False, False)
-        part(1, "s", False, True)
-        part(2, "s", False, True)
-        part(3, "l", False, False)
-        part(3, "w", False, False)
-        part(3, "s", False, True)
+        act(sg, wg, AF.Sign, ["wg"], ["sg"], bias=-31.5)
+        mm(P(1), T.i32[:], lg, True, False, ["i32", "lg"], ["b1"])
+        mm(P(1), T.i1[:], wg, False, False, ["i1", "wg"], ["b1"])
+        mm(P(1), T.in16[:], sg, False, True, ["in16", "sg"], ["b1"])
+        send(1, ro[:], op[:], ["lg", "wg", "sg"], "ao_%d" % t)
+        if t:
+            send(RO - t + 1, T.hb[:, 20 * t:20 * t + 20], T["hs_%d" % t][:, 0:20], ["hsa_%d" % t, "hsb_%d" % t], "ah_%d" % t)
         ts(T.st[:], P(1), -OFD, ADD, ["b1"], ["st"])
-        for j, (lo, hi) in enumerate(SCH):
-            act(T.vv[:, 16 * lo:16 * hi], T.xt[:].indirect(T.st[:, lo:hi]), AF.Copy, ["x", "st"], ["vv%d" % j])
-        cp(T.dru[:], P(2), ["b2"], ["dru"])
-        if t > 0:
-            late[1](m1[:, 10:20], "m1t_%d" % t)
-        ts(T["awm%d" % (t % 2)][:], aw, -16.0 - 4096.0 - 131072.0, ADD, [taw], ["awm%d" % (t % 2)])
-        scan(T.dws[:], T.rsw[:], P(3), MIN, MAX, ["rsw", "b3"], ["dws"])
-        for c in range(10):
-            nn = B - 16 * c
-            e0 = c * B
-            ts(T.eq[:, e0:e0 + nn], T.dru[:, 16 * c:B], T.dws[:, 16 * c + 15:16 * c + 16], EQ, ["dru", "dws"], ["eq%d" % c])
-            mm(b[5][:, 16 * c:B], T.gwa[:, 128 * c:128 * c + 128], T.eq[:, e0:e0 + nn], False, c == 9, ["gw%d" % c, "eq%d" % c], ["b5"])
-        mm(b[0][:, 256:256 + B], T.i1[:], T.y2[:], True, True, ["i1", "y2"], ["b0"])
-        mm(b[6][:, 256:256 + B], T.in1[:], y, True, False, ["in1", ty], ["b6"])
-        mm(P(4), T.ea[:], T.lg[:], False, False, ["ea", "lg"], ["b4"])
-        mm(P(4), T.eb[:], T.lg[:], False, True, ["eb", "lg"], ["b4"])
-        mm(P(7), T.i1[:], T.cg[:], False, False, ["i1", "cg"], ["b7"])
-
-        def min4(j):
-            lo, hi = SCH[j]
-            scan(T.mn[:, 16 * lo:16 * hi], T.rs1[:, 0:16 * (hi - lo)], T.vv[:, 16 * lo:16 * hi], MAX, MIN, RS1 + ["vv%d" % j], ["mn%d" % j])
-
-        def max4(j):
-            lo, hi = SCH[j]
-            scan(T.mx[:, 4 * lo:4 * hi], T.rs2[:, 0:4 * (hi - lo)], T.mn[:, 16 * lo + 3:16 * hi:4], MIN, MAX, ["rs2", "mn%d" % j], ["mx%d" % j])
-        if t:
-            min4(0)
-        else:
-            unit(4)
-        scan(T.rs[:], T.rsw[:], P(5), MIN, MAX, ["rsw", "b5"], ["rs"])
-        if t:
-            max4(0)
-        tt(T.lose[:], T.rs[:, 15:B:16], T.thr[:], GE, ["rs", "thr"], ["lose"])
-        if t:
-            min4(1)
-        tt(T.lose2[:], T.lose[:], T.dum[:], MUL, ["lose", "dum"], ["lose2"])
-        if t:
-            max4(1)
-        tt(T.dd[:], T.lose2[:], T.dws[:, 15:B:16], MAX, ["lose2", "dws"], ["dd"])
-        if t:
-            min4(2)
-        ts(m1[:, 0:10], T.dd[:], -OFD, ADD, ["dd"], ["m1d_%d" % t])
-        wid = 10 if t == 0 else 20
-        send(T["r1_%d" % t][:, 0:wid], m1[:, 0:wid], ["m1d_%d" % t] + (["m1t_%d" % t] if t else []), "a1_%d" % t)
         if t == 0:
-            unit(5)
-            unit(6)
-            min4(0)
-            min4(1)
-            max4(0)
-            max4(1)
-            min4(2)
-        max4(2)
-        min4(3)
-        max4(3)
+            for u in range(3, len(UNITS)):
+                unit(u, True)
+        for lo, hi in SCH:
+            act(T.vv[:, 16 * lo:16 * hi], T.xt[:].indirect(T.st[:, lo:hi]), AF.Copy, ["x", "st"], ["vv%d" % lo])
+        if t == 0:
+            twice(y, ty)
+        lo, hi = VCH
+        cp(T.vv[:, 16 * lo:16 * hi], T.xt[:].indirect(T.st[:, lo:hi]), ["x", "st"], ["vv%d" % lo])
+        mm(P(4), T.i1[:], T.mask[:], True, False, ["i1", "mask"], ["b4"])
+        mm(P(4), T.ea[:], lg, False, False, ["ea", "lg"], ["b4"])
+        mm(P(4), T.eb[:], lg, False, True, ["eb", "lg"], ["b4"])
+        mm(P(7), T.i1[:], T.mask[:], True, False, ["i1", "mask"], ["b7"])
+        mm(P(7), T.i1[:], T.cg[:], False, False, ["i1", "cg"], ["b7"])
+        mm(P(3), T.i1[:], T.mask[:], True, False, ["i1", "mask"], ["b3"])
+        mm(P(5), T.in1[:], T.mask[:], True, False, ["in1", "mask"], ["b5"])
+        mm(P(6), T.in1[:], y, True, False, ["in1", ty], ["b6"])
+        min4(*VCH)
+        min4(*SCH[0])
+        mtok = [max4([VCH])]
+        min4(*SCH[1])
+        mtok.append(max4(SCH[0:1]))
+        min4(*SCH[2])
+        mtok.append(max4(SCH[1:2]))
+        min4(*SCH[3])
+        mtok.append(max4(SCH[2:4]))
         mall = T.mx[:, 3:4 * B:4]
-        mtok = ["mx0", "mx1", "mx2", "mx3"]
-        mm(b[6][:, 256:256 + B], T.i1[:], T.mx[:, 3:4 * B:4], False, True, ["i1", "mx0", "mx1", "mx2", "mx3"], ["b6"])
+        mm(P(6), T.i1[:], mall, False, True, ["i1"] + mtok, ["b6"])
         act(T.kk2[:], mall, AF.Sign, mtok, ["kk2"])
-        act(zs[:], b[6][:, 256:256 + B], AF.Abs, ["b6"], ["zs_%d" % t])
-        send(T["rz_%d" % t][:], zs[:], ["zs_%d" % t], "az_%d" % t)
-        tt(T.kk[:], mall, b[0][:, 256:256 + B], GE, mtok + ["b0"], ["kk"])
+        act(zs[:], P(6), AF.Abs, ["b6"], ["zs_%d" % t])
+        send(1, rz[:], zs[:], ["zs_%d" % t], "az_%d" % t)
+        tt(T.kk[:], mall, P(0), GT, mtok + ["b0"], ["kk"])
         scan(T.ps[:], T.rsw[:], P(4), MIN, MAX, ["rsw", "b4"], ["ps"])
-        ts(T.d0[:, 1:60:6], T.ps[:, 15:B:16], M16K, ADD, ["ps"], ["d0s"], M16K, SUB)
-        tt(T.d1[:, 1:60:6], T.d0[:, 1:60:6], T.ps[:, 15:B:16], SUB, ["d0s", "ps"], ["d1s"])
+        pw = T.ps[:, 15:B:16]
+        act(T.t1[:], pw, AF.Identity, ["ps"], ["t1"], bias=M16K)
+        act(T.d1[:, 1:60:6], pw, AF.Identity, ["ps"], ["d1s"], scale=-1.0, bias=-14.5)
+        act(T.d0[:, 1:60:6], T.t1[:], AF.Identity, ["t1"], ["d0s"], scale=1.0 / 512.0, bias=-M16K / 512.0)
+
+        def place(j, first):
+            for k, lhs in enumerate(("e15x", "e15", "e15n")):
+                mm(P(j), T[lhs][:], ro[:, B * k:B * k + B], first and k == 0, j != 5 and k == 2, [lhs, "ro_%d" % t], ["b%d" % j])
+        place(3, False)
         mm(P(7), T.gb[:], T.kk2[:], False, False, ["g8n", "kk2"], ["b7"])
         mm(P(7), T.g8[:], T.kk[:], False, False, ["g8", "kk"], ["b7"])
         mm(P(7), T.g1[:], zs[:], False, True, ["g1", "zs_%d" % t], ["b7"])
+        place(2, True)
+        place(6, True)
+        place(5, False)
+
+        def same(c):
+            ts(T.eq[:, c * B + 16 * c:c * B + B], b[2][:, 16 * c:B], T.dws[:, 16 * c - 1:16 * c], EQ, ["b2", "dws"], ["eq%d" % c])
+
+        def count(c, src, tok, stop=False):
+            mm(b[5][:, 16 * c:B], T.g8[:], src, False, stop, ["g8", tok], ["b5"])
+        scan(T.dws[:], T.rsw[:], P(3), MIN, MAX, ["rsw", "b3"], ["dws"])
         scan(T.qs[:], T.rsw[:], P(7), MIN, MAX, ["rsw", "b7"], ["qs"])
         q = T.qs[:, 15:B:16]
-        act(T.d1[:, 2:60:6], q, AF.Identity, ["qs", "ac0"], ["d1x1"], bias=T.ac[:, 0:1])
-        act(T.d1[:, 5:60:6], q, AF.Identity, ["qs", "ac1"], ["d1x2"], bias=T.ac[:, 1:2])
+        am, tam = T.am[:, t:t + 1], "am%d" % t
+        ts(T.raw[:], T.dws[:, 15:B:16], -OFD, ADD, ["dws"], ["raw"])
+        ts(T.d1[:, 0:60:6], q, -7.0 * 8192.0 - 0.5, GE, ["qs"], ["d1b"], 512.0, ADD)
+        toks = ["d0c", "d0s", "d1c", "d1s", "d1b", "d1x0", "d1x1", "d1x2", "d1x3"]
+        act(T.d1[:, 2:60:6], q, AF.Identity, ["qs", tam], ["d1x0"], bias=am)
         if not last:
-            act(T.d1[:, 62:120:6], q, AF.Identity, ["qs", "ac2"], ["d1x3"], bias=T.ac[:, 2:3])
-        ts(T.d1[:, 0:60:6], q, 73711.5 - 131072.0, GE, ["qs"], ["d1b"], 1.0 / 512.0, MUL)
-
-        h = t % 2
-        am, awm, tam, tawm = T.am[:, h:h + 1], T["awm%d" % h][:], "am%d" % h, "awm%d" % h
-
-        def clock1(q=q, am=am, awm=awm, tam=tam, tawm=tawm, tfin=tfin, ttf=ttf):
-            tt(T.qi[:], q, awm, SUB, ["qs", tawm], ["qi"])
-            ts(T.tfa[:], tfin, am, ADD, [ttf, tam], ["tfa"], 1.0, ADD)
-            ts(T.qi2[:], T.qi[:], 31, AND, ["qi"], ["qi2"])
-
-        def clock2(out, tok):
-            tt(T.tfn[:], T.tfa[:], T.qi2[:], ADD, ["tfa", "qi2"], ["tfn"])
-            cp(out, T.tfn[:], ["tfn"], [tok])
-        toks = ["d0c", "d0s", "d1c", "d1s", "d1b", "d1x1", "d1x2"]
-        if last:
-            scan(T.po[:, 0:60], T.d0[:, 0:60], T.d1[:, 0:60], MUL, ADD, toks, ["po"])
-            ts(m3[:, 0:10], T.po[:, 5:60:6], -OFF, ADD, ["po"], ["m3a"])
-            clock1()
-            clock2(m3[:, 10:20], "m3b")
-            send(T["r3_%d" % t][:], m3[:], ["m3a", "m3b"], "a3_%d" % t)
+            act(T.d1[:, 5:60:6], q, AF.Identity, ["qs", tam], ["d1x1"], bias=am)
+            act(T.d1[:, 62:120:6], q, AF.Identity, ["qs", tam], ["d1x2"], bias=am)
+            ts(T.d1[:, 65:120:6], q, am, ADD, ["qs", tam], ["d1x3"])
+            same(9)
+            scan(T.po[:], T.d0[:], T.d1[:], MUL, ADD, toks, ["po"])
+            same(8)
+            ts(m3[:], T.po[:, 5:120:6], 1.0 - OFF, ADD, ["po"], ["m3_%d" % t])
+            send(1, T["r3_%d" % t][:], m3[:], ["m3_%d" % t], "a3_%d" % t)
+            mm(b[1][:, 256:266], T.onef[:], T.d1[:, 0:60:6], True, True, ["onef", "d1b"], ["b1"])
         else:
-            tt(T.d1[:, 65:120:6], q, T.ta4[:], ADD, ["qs", "ta4"], ["d1x4"])
-            scan(T.po[:], T.d0[:], T.d1[:], MUL, ADD, toks + ["d1x3", "d1x4"], ["po"])
-            ts(m3[:], T.po[:, 5:120:6], -OFF, ADD, ["po"], ["m3_%d" % t])
-            send(T["r3_%d" % t][:], m3[:], ["m3_%d" % t], "a3_%d" % t)
-            mm(b[0][:, 0:10], T.one5[:], T.d1[:, 0:60:6], True, True, ["one5", "d1b"], ["b0"])
-            if t == 0:
-                unit(7)
-            do("V", lambda v: v.tensor_reduce(T.acol[:], b[0][:, 0:10], AxisListType.X, ADD), ["b0"], ["acol"])
-            for j, v in enumerate(AC):
-                act(T.ac[:, j:j + 1], T.acol[:], AF.Identity, ["acol"], ["ac%d" % j], bias=v, scale=1.0)
-            act(T.ta4[:], T.li16[:], AF.Identity, ["li16", "acol"], ["ta4"], bias=T.acol[:], scale=1.0)
-            act(T.am1[:], T.acol[:], AF.Identity, ["acol"], ["am1"], bias=-15.5, scale=1.0)
-            act(T.am2[:], T.am1[:], AF.Identity, ["am1"], ["am2"], bias=M32, scale=1.0)
-            act(T.am3[:], T.am2[:], AF.Identity, ["am2"], ["am3"], bias=-M32, scale=1.0)
-            act(T.am[:, 1 - h:2 - h], T.am3[:], AF.Identity, ["am3", "acol"], ["am%d" % (1 - h)], bias=T.acol[:], scale=-1.0)
-        late = (clock1, clock2)
-        rewrite_prep(t + 1)
-        if not last:
-            clock1()
-    rewrite(RO)
+            same(9)
+            scan(T.po[:, 0:60], T.d0[:, 0:60], T.d1[:, 0:60], MUL, ADD, toks, ["po"])
+            same(8)
+        seg = [0]
+        for c in range(1, NS + 1):
+            seg.append(seg[-1] + B - 16 * c)
+            act(T.ab[:, seg[c - 1]:seg[c]], b[6][:, 16 * c:B], AF.Abs, ["b6", "dws"], ["ab%d" % c], scale=-1.0, bias=T.dws[:, 16 * c - 1:16 * c])
+        act(T.es[:, 0:seg[NS]], T.ab[:, 0:seg[NS]], AF.Relu, ["ab%d" % c for c in range(1, NS + 1)], ["es"], scale=-1.0, bias=1.0)
+        tt(T.eq[:, 1:B], b[2][:, 1:B], T.dws[:, 0:B - 1], EQ, ["b2", "dws"], ["eqd"])
+        for c in range(7, NS, -1):
+            same(c)
+        for c in range(9, NS, -1):
+            count(c, T.eq[:, c * B + 16 * c:c * B + B], "eq%d" % c)
+            if c == 8:
+                mm(b[5][:, 1:B], T.g8[:], T.eq[:, 1:B], False, False, ["g8", "eqd"], ["b5"])
+        for c in range(1, NS + 1):
+            count(c, T.es[:, seg[c - 1]:seg[c]], "es", c == NS)
+        act(hs[:, 0:10], q, AF.Identity, ["qs"], ["hsa_%d" % (t + 1)], bias=-float(t))
+        act(hs[:, 10:20], T.d1[:, 2:60:6], AF.Identity, ["d1x0"], ["hsb_%d" % (t + 1)], bias=-float(t))
+        if last:
+            act(hs[:, 20:30], T.po[:, 1:60:6], AF.Identity, ["po"], ["hsc"], scale=-0.03125, bias=-136.0 - 14.5 / 32.0)
+            send(1, T.hb[:, 80:110], hs[:], ["hsa_4", "hsb_4", "hsc"], "ah_4")
+        else:
+            act(T.junk[:], b[1][:, 256:266], AF.Identity, ["b1"], ["junk", "am%d" % (t + 1)], bias=-65536.0, accum_out=T.am[:, t + 1:t + 2])
+            twice(rz[:], "rz_%d" % t)
+        tt(T.ui[:], T.wy[:].indirect(T.raw[:]), rz[:], ADD, WY + ["raw", "rz_%d" % t], ["ui"])
+        scan(T.rs[:], T.dumr[:], P(5), MAX, MIN, ["dumr", "b5"], ["rs"])
+        ts(T.ui2[:], T.ui[:], 31, AND, ["ui"], ["ui2"])
+        ts(T.dst[:], T.rs[:, 15:B:16], -OFD, ADD, ["rs"], ["dst"])
+        cp(T.wy[:].indirect(T.dst[:]), T.ui2[:], ["ui2", "dst"], WY)
     dma("Y", T.yw[:], T.wy[:, 0:W], WY, [], "oyw")
     dma("S", T.yy[:], T["rz_3"][:], ["rz_3"], [], "oyy")
-    cp(T.fi[:], T["r3_3"][:], ["r3_3"], ["fi"])
-    ts(T.fi2[:, 0:10], T.fi[:, 0:10], 5, SHR, ["fi"], ["fi2a"])
-    ts(T.fi2[:, 10:20], T.fi[:, 10:20], 4095, AND, ["fi"], ["fi2b"])
-    cp(T.ft[:, 0:20], T.fi2[:], ["fi2a", "fi2b"], ["ft"])
-    do("V", lambda v: v.transpose(T.ftt[:], T.ft[:]), ["ft"], ["ftt"])
-    for a in range(4):
-        for h in range(2):
-            r = 2 * a + h
-            dma("S", T.yl[r:r + 1, :], T.ftt[32 * a:32 * a + 10, 16 * h:16 * h + 16], ["ftt"], [], "osm")
-            dma("Y", T.yt[r:r + 1, :], T.ftt[32 * a + 10:32 * a + 20, 16 * h:16 * h + 16], ["ftt"], [], "osn")
+    HB = ["hb%d" % t for t in range(RO + 1)]
+    for t in range(RO + 1):
+        arrives(RO - max(t - 1, 0), HB[t], "ah_%d" % t)
+    tt(T.fa[:], T.hb[:, 20:100], T.hb[:, 10:90], SUB, HB, ["fa"])
+    ts(T.fb[:], T.fa[:], 31, AND, ["fa"], ["fb"])
+    tt(T.fc[:], T.fb[:, 0:40], T.fb[:, 40:80], ADD, ["fb"], ["fc"])
+    tt(T.fd[:], T.fc[:, 0:20], T.fc[:, 20:40], ADD, ["fc"], ["fd"])
+    tt(T.fe[:], T.fd[:, 0:10], T.hb[:, 0:10], ADD, ["fd"], ["fe"])
+    tt(T.ff[:], T.fd[:, 10:20], T.fe[:], ADD, ["fd", "fe"], ["ff"])
+    ts(T.fg[:], T.ff[:], 4095, AND, ["ff"], ["fg"])
+    cp(T.hb[:, 110:120], T.fg[:], ["fg"], ["hbt"])
+    for p in range(16):
+        mm(b[1][0:8, p:2 * B:16], T.idf[:, p:128:16], T.hb[:, 100:120], True, True, ["idf", "hbt"] + HB, ["b1"])
+    cp(T.fin[:], b[1][0:8, 0:2 * B], ["b1"], ["fin"])
+    dma("S", T.yl[:], T.fin[:, 0:B], ["fin"], [], "osm")
+    dma("Y", T.yt[:], T.fin[:, B:2 * B], ["fin"], [], "osn")
     g.wait_ge(T.sem.loc, sent[0])
     for s, v in tot.items():
         if know["P"].get(s, 0) < v:

@@ -1,43 +1,49 @@
 from concourse.mybir import AluOpType, ActivationFunctionType
 
 W, B, RO = 3712, 160, 4
-PIECES = [(0, 2208), (2208, W)]
-UNITS = [(0, 736), (736, 1472), (1472, 2208), (2208, 2712), (2712, 3216), (3216, W)]
-VCH = (0, 40)
-SCH = [(40, 88), (88, 128), (128, 152), (152, 160)]
+PIECES = [(0, 1856), (1856, W)]
+UNITS = [(0, 928), (928, 1856), (1856, 2464), (2464, 3072), (3072, W)]
+SCH = [(48, 92), (92, 130), (130, 152), (152, 160)]
+VCH = [("g", 0, 24), ("g", 24, 48), ("n", 0, 24), ("n", 48, 92), ("n", 24, 48), ("n", 92, 130), ("x", 0, 92), ("n", 130, 152),
+       ("x", 92, 130), ("n", 152, 160), ("x", 130, 160)]
 OFF = 4352.0
-OFD = OFF + 16.0
-NS = 4
+OFS = OFF - 32.0
+MID = 1856.0
+NF, NL = 2, 2
+WV = False
+EO = 2
+LP = 6
 M32 = 402653184.0
 M16 = 201326592.0
 M16K = 1.5 * 2.0 ** 37
 
-F32, BF, I32, U16 = "float32", "bfloat16", "int32", "uint16"
+F32, BF, F16, I32, U16 = "float32", "bfloat16", "float16", "int32", "uint16"
 SCRATCH = {}
 for _dt, _rows, _list in (
     (I32, 128, {"ilt": W, "tmp": W, "wgi": B, "ui": B, "ui2": B, "pq": B, "pq2": B, "pm0": 10, "pm": 10, "c16": 10,
-                "fa": 80, "fb": 80, "fc": 40, "fd": 20, "fe": 10, "ff": 10, "fg": 10}),
-    (BF, 128, {"xt": W, "wy": W + B, "colt": W, "vv": 16 * B, "mn": 16 * B, "mx": 4 * B, "eq": 10 * B, "y0t": B, "cg": B, "kk": B, "kk2": B,
-               "ones": 224, "g1": 128, "gb": 128, "i1": 128, "i32": 128, "in1": 128, "g8": 128, "e15": 128, "e15x": 128, "e15n": 128,
-               "ea": 128, "eb": 128, "e0": 128, "e0x": 128, "mask": B, "ab": 4 * B, "es": 4 * B, "in16": 128, "e15m": 128, "rs1": 768, "rs2": 224}),
+                "fa": 60, "fb": 60, "fh": 10, "fi": 10}),
+    (BF, 128, {"xt": W, "wy": W + B, "colt": W, "vv": 16 * B, "mn": 16 * B, "mx": 4 * B, "eq": 10 * B, "y0t": B, "kk": B, "kk2": B,
+               "lg": B, "wg": B, "cn": B, "cy": B, "ones": B, "g1": 128, "g8n": 128, "i1": 128, "i32": 128, "in1": 128, "in32": 128, "g8": 128,
+               "eb": 128, "e0x": 128, "e1x": 128, "jr": 128, "ja": 128, "mask": B, "ab": 6 * B, "es": 6 * B, "rs1": 768, "rs2": 384, "fc": 60}),
     (F32, 128, {"dws": B, "ps": B, "rs": B, "qs": B, "q16": B, "rsw": B, "dumr": B, "d0": 120, "d1": 120, "po": 120, "t1": 10, "li": 10,
-                "am": 4, "junk": 10, "onef": 128, "idf": 128, "hb": 120}),
+                "am": 8, "junk": 10, "onef": 128, "idf": 128, "hb": 110}),
+    (F16, 128, {"e15": 128}),
     (U16, 128, {"st": B, "aw0": 10, "raw": 10, "dst": 10}),
     (I32, 8, {"ln8": B, "tk8": B, "ti8": B, "th8": B}),
     (BF, 8, {"lb8": B, "tb8": B, "tc8": B, "sel": 128, "sel32": 128}),
-    (F32, 8, {"fin": 2 * B}),
+    (F32, 8, {"fl": B, "ft": B}),
 ):
     for _k, _n in _list.items():
         SCRATCH[_k] = ("sbuf", [_rows, _n], _dt)
 for _t in range(RO):
     for _k in ("op", "ro"):
-        SCRATCH["%s_%d" % (_k, _t)] = ("sbuf", [128, 3 * B], BF)
+        SCRATCH["%s_%d" % (_k, _t)] = ("sbuf", [128, B], F16)
     for _k in ("zs", "rz"):
         SCRATCH["%s_%d" % (_k, _t)] = ("sbuf", [128, B], BF)
     for _k in ("m3", "r3"):
         SCRATCH["%s_%d" % (_k, _t)] = ("sbuf", [128, 20], U16)
 for _t in range(RO + 1):
-    SCRATCH["hs_%d" % _t] = ("sbuf", [128, 30], F32)
+    SCRATCH["hs_%d" % _t] = ("sbuf", [128, 20], F32)
 for _t in range(8):
     SCRATCH["b%d" % _t] = ("psum", [128, 512], F32)
 SEMAPHORES = ["qV", "qS", "qT", "qP", "loc", "dil0", "dil1", "dx", "dy", "dln", "dtk", "oyy", "oyw", "osm", "osn"]
@@ -50,7 +56,7 @@ def rank_program(g, core, T, topo):
         return
     n = len(T.cores)
     OP, AF = AluOpType, ActivationFunctionType
-    ADD, SUB, MUL, MAX, MIN, EQ, GE, GT = OP.add, OP.subtract, OP.mult, OP.max, OP.min, OP.is_equal, OP.is_ge, OP.is_gt
+    ADD, SUB, MUL, MAX, MIN, EQ, GE, GT, LT = OP.add, OP.subtract, OP.mult, OP.max, OP.min, OP.is_equal, OP.is_ge, OP.is_gt, OP.is_lt
     AND, SHR = OP.bitwise_and, OP.arith_shift_right
     eng = {"V": g.vector, "S": g.scalar, "T": g.tensor, "P": g, "Y": g.sync}
     know = {e: {} for e in eng}
@@ -106,6 +112,9 @@ def rank_program(g, core, T, topo):
     def cp(out, a, r, w):
         do("V", lambda v: v.tensor_copy(out, a), r, w)
 
+    def ms(ap, val, w):
+        do("V", lambda v: v.memset(ap, val), [], [w])
+
     def scan(out, x0, x1, o0, o1, r, w):
         do("V", lambda v: v.tensor_tensor_scan(out, x0, x1, 0.0, o0, o1), r, w)
 
@@ -142,38 +151,41 @@ def rank_program(g, core, T, topo):
     dma("Y", T.xt[:], T.xw[:], [], ["x"], "dx")
     dma("Y", T.y0t[:], T.y0[:], [], ["y0"], "dy")
 
-    do("V", lambda v: v.memset(T.ones[:], 1.0), [], ["ones"])
+    small = {"allow_small_or_imprecise_dtypes": True}
+    ms(T.ones[:], 1.0, "ones")
     pool(lambda p: p.iota(T.pq[:], [[0, 10], [1, 16]], 128, -1), [], ["pq"])
-    pool(lambda p: p.iota(T.q16[:], [[0, 10], [1, 16]], 0, 0, allow_small_or_imprecise_dtypes=True), [], ["q16"])
+    pool(lambda p: p.iota(T.q16[:], [[0, 10], [1, 16]], 0, 0, **small), [], ["q16"])
     pool(lambda p: p.affine_select(T.i1[:], T.ones[:, 0:128], [[-1, 128]], EQ, 0.0, 0, 1), ["ones"], ["i1"])
     pool(lambda p: p.affine_select(T.sel[:], T.ones[0:8, 0:128], [[1, 8], [0, 16]], EQ, 0.0, 0, -1), ["ones"], ["sel"])
+    pool(lambda p: p.iota(T.colt[:, 0:928], [[0, 29], [-1, 32]], 32, 0, **small), [], ["colt0"])
+    pool(lambda p: p.iota(T.jr[:], [[-16, 8], [0, 16]], 0, 1, **small), [], ["jr"])
     pool(lambda p: p.iota(T.pm0[:], [[0, 10]], 0, 1), [], ["pm0"])
     pool(lambda p: p.iota(T.c16[:], [[16, 10]], 0, 0), [], ["c16"])
-    pool(lambda p: p.iota(T.colt[:, 0:928], [[0, 29], [1, 32]], 0, 0, allow_small_or_imprecise_dtypes=True), [], ["colt0"])
-    pool(lambda p: p.affine_select(T.gb[:], T.ones[:, 0:128], [[-16, 8], [0, 16]], GE, 0.0, 0, 1), ["ones"], ["gb"])
-    pool(lambda p: p.affine_select(T.g1[:], T.gb[:], [[16, 8], [0, 16]], GE, 0.0, 15, -1), ["gb"], ["g1"])
+    CT = ["colt%d" % j for j in range(4)]
 
     def fill(ap, n_, v, w):
         act(ap, T.ones[:, 0:n_], AF.Copy, ["ones"], [w], scale=v)
     fill(T.d0[:], 120, 1.0, "d0c")
+    fill(T.d1[:], 120, 0.0, "d1c")
+    fill(T.dumr[:], B, -4096.0, "dumr")
     for lo, v in ((0, 0.0), (5, -1.0)):
         fill(T.d0[:, lo:120:6], 20, v, "d0c")
-    fill(T.d1[:], 120, 0.0, "d1c")
     for lo, hi, v in ((3, 60, M32), (4, 60, -M32), (63, 120, M16), (64, 120, -M16)):
         fill(T.d1[:, lo:hi:6], 10, v, "d1c")
     for k in ("d1b", "d1s", "d1x0", "d1x1", "d1x2", "d1x3"):
         lastw[k] = lastw["d1c"]
     lastw["d0s"] = lastw["d0c"]
-    fill(T.rs2[:], 224, 0.0, "rs2")
-    fill(T.dumr[:], B, 0.0, "dumr")
-    Q4 = [[0, 56], [1, 4]]
-    pool(lambda p: p.affine_select(T.rs1[:, 0:192], T.rs2[:, 0:192], [[0, 48], [1, 4]], OP.not_equal, 512.0, 0, 0), ["rs2"], ["rs1_0"])
-    pool(lambda p: p.affine_select(T.rs2[:], T.rs2[:], Q4, EQ, 512.0, 0, 0), ["rs2"], ["rs2"])
-    CT = ["colt%d" % j for j in range(4)]
+    fill(T.am[:, 0:1], 1, 0.0, "am0")
+    fill(T.onef[:], 128, 1.0, "onef")
+    fill(T.wy[:, W:W + B], B, 0.0, "wyd")
+    ms(T.rs1[:], 0.0, "rs1")
+    ms(T.rs2[:], 512.0, "rs2")
+    ms(T.rs1[:, 0:768:4], 512.0, "rs1")
+    ms(T.rs2[:, 0:384:4], 0.0, "rs2")
 
     ts(T.pq2[:], T.pq[:], 15, AND, ["pq"], ["pq2"])
-    ts(T.mask[:], T.pq2[:], 0.0, GT, ["pq2"], ["mask"], -(2.0 ** 60), MUL)
     ts(T.rsw[:], T.q16[:], -0.5, ADD, ["q16"], ["rsw"], 1e27, MUL)
+    ts(T.mask[:], T.pq2[:], 0.0, GT, ["pq2"], ["mask"], -(2.0 ** 60), MUL)
     act(T.sel32[:], T.sel[:], AF.Copy, ["sel"], ["sel32"], scale=32.0)
     cp(T.lb8[:], T.ln8[:], ["ln8"], ["lb8"])
     ts(T.ti8[:], T.tk8[:], 31, AND, ["tk8"], ["ti8"])
@@ -185,70 +197,56 @@ def rank_program(g, core, T, topo):
         mm(P(j), T.sel32[:], T[hi][:], False, False, ["sel32", hi], ["b%d" % j])
         mm(P(j), T.sel[:], T.tb8[:], False, True, ["sel", "tb8"], ["b%d" % j])
     scan(T.qs[:], T.rsw[:], P(0), MIN, MAX, ["rsw", "b0"], ["qs"])
-    cp(T.aw0[:], T.qs[:, 15:B:16], ["qs"], ["aw_0"])
     scan(T.ps[:], T.rsw[:], P(1), MIN, MAX, ["rsw", "b1"], ["ps"])
+    cp(T.aw0[:], T.qs[:, 15:B:16], ["qs"], ["aw_0"])
+    for k, v in (("i32", 32.0), ("in1", -1.0), ("in32", -32.0), ("idf", 1.0)):
+        act(T[k][:], T.i1[:], AF.Copy, ["i1"], [k], scale=v)
     act(T.hs_0[:, 0:10], T.ps[:, 15:B:16], AF.Identity, ["ps"], ["hsa_0"], bias=float(RO))
     act(T.hs_0[:, 10:20], T.ps[:, 15:B:16], AF.Copy, ["ps"], ["hsb_0"])
-
-    GP = [[-16, 8], [0, 16]]
-    pool(lambda p: p.affine_select(T.e15[:], T.ones[:, 0:128], GP, EQ, 0.0, -15, 1), ["ones"], ["e15"])
-    pool(lambda p: p.affine_select(T.e0[:], T.ones[:, 0:128], GP, EQ, 0.0, 0, 1), ["ones"], ["e0"])
-    act(T.i32[:], T.i1[:], AF.Copy, ["i1"], ["i32"], scale=32.0)
-    act(T.in1[:], T.i1[:], AF.Copy, ["i1"], ["in1"], scale=-1.0)
+    send(RO, T.hb[:, 0:20], T.hs_0[:, 0:20], ["hsa_0", "hsb_0"], "ah_0")
+    act(T.ja[:], T.jr[:], AF.Abs, ["jr"], ["ja"], bias=-7.5)
     for j in range(1, 4):
         act(T.colt[:, 928 * j:928 * j + 928], T.colt[:, 0:928], AF.Copy, ["colt0"], ["colt%d" % j])
-    act(T.e15x[:], T.e15[:], AF.Copy, ["e15"], ["e15x"], scale=32.0)
-    act(T.e15n[:], T.e15[:], AF.Copy, ["e15"], ["e15n"], scale=-16.0)
-    act(T.in16[:], T.i1[:], AF.Copy, ["i1"], ["in16"], scale=-16.0)
-    act(T.e0x[:], T.e0[:], AF.Copy, ["e0"], ["e0x"], scale=16384.0)
-    pool(lambda p: p.affine_select(T.ea[:], T.e0x[:], GP, OP.not_equal, -16384.0, -1, 1), ["e0x"], ["ea"])
-    send(RO, T.hb[:, 0:20], T.hs_0[:, 0:20], ["hsa_0", "hsb_0"], "ah_0")
-    act(T.eb[:], T.e0[:], AF.Copy, ["e0"], ["eb"], scale=32.0)
-    act(T.g8[:], T.g1[:], AF.Copy, ["g1"], ["g8"], scale=8192.0)
-    act(T.gb[:], T.g1[:], AF.Copy, ["g1", "gb"], ["g8n"], scale=-8192.0)
+
+    for k, row, v in (("e15", 15.0, 1.0), ("eb", 0.0, 32.0), ("e0x", 0.0, 16384.0), ("e1x", 1.0, -16384.0)):
+        ts(T[k][:], T.jr[:], row, EQ, ["jr"], [k], v, MUL)
     ts(T.pm[:], T.pm0[:], 15, AND, ["pm0"], ["pm"])
+    for k, v in (("g1", 1.0), ("g8", 8192.0), ("g8n", -8192.0)):
+        ts(T[k][:], T.ja[:], 8.0, LT, ["ja"], [k], v, MUL)
     tt(T.li[:], T.pm[:], T.c16[:], ADD, ["pm", "c16"], ["li"])
     act(T.d1[:, 60:120:6], T.li[:], AF.Identity, ["li"], ["d1c"], bias=-OFF - 6.5, scale=-16.0)
-    act(T.dumr[:, 0:B:16], T.li[:], AF.Identity, ["li"], ["dumr"], bias=W + OFD)
-    fill(T.am[:], 4, 0.0, "am0")
-    fill(T.onef[:], 128, 1.0, "onef")
-    act(T.idf[:], T.i1[:], AF.Copy, ["i1"], ["idf"])
-    fill(T.wy[:, W:W + B], B, 0.0, "wyd")
-    for j in range(1, 4):
-        act(T.rs1[:, 192 * j:192 * j + 192], T.rs1[:, 0:192], AF.Copy, ["rs1_0"], ["rs1_%d" % j])
-    RS1 = ["rs1_%d" % j for j in range(4)]
+    act(T.dumr[:, 0:B:16], T.li[:], AF.Identity, ["li"], ["dumr"], bias=W - MID)
 
     WY = ["wy%d" % u for u in range(len(UNITS))] + ["wyd"]
     IL = ["il0", "il1"]
 
-    def unit(u, on_pool=False):
+    def low5(u):
         lo, hi = UNITS[u]
         ts(T.tmp[:, lo:hi], T.ilt[:, lo:hi], 31, AND, ["il%d" % (lo >= PIECES[1][0])], ["tmp%d" % u])
-        if on_pool:
-            pool(lambda p: p.affine_select(T.wy[:, lo:hi], T.tmp[:, lo:hi], [[0, hi - lo]], GE, 0.0, 0, 0), ["tmp%d" % u], ["wy%d" % u])
-        else:
-            cp(T.wy[:, lo:hi], T.tmp[:, lo:hi], ["tmp%d" % u], ["wy%d" % u])
 
-    for u in range(3):
-        unit(u)
+    def narrow(u):
+        lo, hi = UNITS[u]
+        pool(lambda p: p.affine_select(T.wy[:, lo:hi], T.tmp[:, lo:hi], [[0, hi - lo]], GE, 0.0, 0, 0), ["tmp%d" % u], ["wy%d" % u])
+
+    for u in range(2):
+        low5(u)
+        narrow(u)
 
     def twice(y, ty):
         act(P(0), y, AF.Relu, [ty], ["b0"], scale=2.0, bias=-1.0)
 
-    def min4(lo, hi):
-        scan(T.mn[:, 16 * lo:16 * hi], T.rs1[:, 0:16 * (hi - lo)], T.vv[:, 16 * lo:16 * hi], MAX, MIN, RS1 + ["vv%d" % lo], ["mn%d" % lo])
+    def lanes(k, lo, hi):
+        return ["%s%d" % (k, i) for i in range(lo, hi, 2)]
 
-    def max4(chunks):
-        lo, hi = chunks[0][0], chunks[-1][1]
-        scan(T.mx[:, 4 * lo:4 * hi], T.rs2[:, 0:4 * (hi - lo)], T.mn[:, 16 * lo + 3:16 * hi:4], MIN, MAX,
-             ["rs2"] + ["mn%d" % c[0] for c in chunks], ["mx%d" % lo])
-        return "mx%d" % lo
+    HB = ["hb%d" % t for t in range(RO + 1)]
+    for t in range(RO + 1):
+        arrives(RO - max(t - 1, 0), HB[t], "ah_%d" % t)
 
     for t in range(RO):
         last = t == RO - 1
-        op, zs, m3, ro, rz, hs = (T[k % t] for k in ("op_%d", "zs_%d", "m3_%d", "ro_%d", "rz_%d", "hs_%d"))
+        NS = NL if last else NF
+        op, zs, m3, ro, rz = (T[k % t] for k in ("op_%d", "zs_%d", "m3_%d", "ro_%d", "rz_%d"))
         hs = T["hs_%d" % (t + 1)]
-        lg, wg, sg = op[:, 0:B], op[:, B:2 * B], op[:, 2 * B:3 * B]
         if t == 0:
             y, ty, aw, taw = T.y0t[:], "y0", T.aw0[:], "aw_0"
         else:
@@ -258,143 +256,231 @@ def rank_program(g, core, T, topo):
         arrives(1, "rz_%d" % t, "az_%d" % t)
         if not last:
             arrives(1, "r3_%d" % t, "a3_%d" % t)
-        act(T.cg[:], T.colt[:].indirect(aw), AF.Copy, CT + [taw], ["cg"])
-        act(lg, T.ilt[:].indirect(aw), AF.Identity, IL + [taw], ["lg"], scale=0.03125, bias=136.0 - 31.0 / 64.0)
+
+        def words():
+            cp(T.xt[:, 0:16 * B].indirect(T["r3_%d" % (t - 1)][:, 10:20]), y, [ty, taw], ["x"])
+        act(T.cn[:], T.colt[:].indirect(aw), AF.Copy, CT + [taw], ["cn"])
+        act(T.lg[:], T.ilt[:].indirect(aw), AF.Identity, IL + [taw], ["lg"], scale=0.03125, bias=136.0 - 31.0 / 64.0)
+        if t and not WV:
+            act(T.wg[:], T.wy[:].indirect(aw), AF.Copy, WY + [taw], ["wg"])
         if t == 0:
             ts(T.wgi[:], T.ilt[:].indirect(aw), 31, AND, IL + [taw], ["wgi"])
-            tt(wg, T.wgi[:], T.cg[:], ADD, ["wgi", "cg"], ["wg"])
+            low5(2)
+            cp(T.wg[:], T.wgi[:], ["wgi"], ["wg"])
+            tt(T.cy[:], T.wgi[:], T.cn[:], GE, ["wgi", "cn"], ["cy"])
+            low5(3)
+        elif WV:
+            cp(T.wg[:], T.wy[:].indirect(aw), WY + [taw], ["wg"])
+            tt(T.cy[:], T.wg[:], T.cn[:], GE, ["wg", "cn"], ["cy"])
+            words()
         else:
-            tt(wg, T.wy[:].indirect(aw), T.cg[:], ADD, WY + [taw, "cg"], ["wg"])
-            cp(T.xt[:, 0:16 * B].indirect(T["r3_%d" % (t - 1)][:, 10:20]), y, [ty, taw], ["x"])
-        act(sg, wg, AF.Sign, ["wg"], ["sg"], bias=-31.5)
-        mm(P(1), T.i32[:], lg, True, False, ["i32", "lg"], ["b1"])
-        mm(P(1), T.i1[:], wg, False, False, ["i1", "wg"], ["b1"])
-        mm(P(1), T.in16[:], sg, False, True, ["in16", "sg"], ["b1"])
-        send(1, ro[:], op[:], ["lg", "wg", "sg"], "ao_%d" % t)
+            tt(T.cy[:], T.wy[:].indirect(aw), T.cn[:], GE, WY + [taw, "cn"], ["cy"])
+            words()
+        for k, (lhs, rhs) in enumerate((("in1", "cn"), ("i32", "lg"), ("i1", "wg"), ("in32", "cy"))):
+            mm(P(1), T[lhs][:], T[rhs][:], k == 0, k == 3, [lhs, rhs], ["b1"])
+        ts(T.st[:], P(1), -OFS, ADD, ["b1"], ["st"])
+        ts(op[:], P(1), -OFS - MID, ADD, ["b1"], ["op"])
+        send(1, ro[:], op[:], ["op"], "ao_%d" % t)
         if t:
-            send(RO - t + 1, T.hb[:, 20 * t:20 * t + 20], T["hs_%d" % t][:, 0:20], ["hsa_%d" % t, "hsb_%d" % t], "ah_%d" % t)
-        ts(T.st[:], P(1), -OFD, ADD, ["b1"], ["st"])
-        if t == 0:
-            for u in range(3, len(UNITS)):
-                unit(u, True)
+            send(RO - t + 1, T.hb[:, 20 * t:20 * t + 20], T["hs_%d" % t][:], ["hsa_%d" % t, "hsb_%d" % t], "ah_%d" % t)
+        else:
+            low5(4)
+            narrow(2)
+            narrow(3)
         for lo, hi in SCH:
-            act(T.vv[:, 16 * lo:16 * hi], T.xt[:].indirect(T.st[:, lo:hi]), AF.Copy, ["x", "st"], ["vv%d" % lo])
+            act(T.vv[:, 16 * lo:16 * hi], T.xt[:].indirect(T.st[:, lo:hi]), AF.Copy, ["x", "st"], lanes("vv", lo, hi))
         if t == 0:
             twice(y, ty)
-        lo, hi = VCH
-        cp(T.vv[:, 16 * lo:16 * hi], T.xt[:].indirect(T.st[:, lo:hi]), ["x", "st"], ["vv%d" % lo])
+        if last:
+            for k, (lo, v) in enumerate(((60, -15.5), (63, M32), (64, -M32))):
+                act(T.am[:, 4 + k:5 + k], T.am[:, 3 + k:4 + k], AF.Identity, ["am%d" % (3 + k)], ["am%d" % (4 + k)], bias=v)
+                act(T.d1[:, lo:120:6], T.ones[:, 0:10], AF.Copy, ["ones", "po"], ["d1c%d" % k], scale=v)
+            act(T.am[:, 7:8], T.am[:, 6:7], AF.Identity, ["am6", "am3"], ["am7"], scale=-1.0, bias=T.am[:, 3:4])
         mm(P(4), T.i1[:], T.mask[:], True, False, ["i1", "mask"], ["b4"])
-        mm(P(4), T.ea[:], lg, False, False, ["ea", "lg"], ["b4"])
-        mm(P(4), T.eb[:], lg, False, True, ["eb", "lg"], ["b4"])
+        for k in ("e0x", "e1x", "eb"):
+            mm(P(4), T[k][:], T.lg[:], False, k == "eb", [k, "lg"], ["b4"])
         mm(P(7), T.i1[:], T.mask[:], True, False, ["i1", "mask"], ["b7"])
-        mm(P(7), T.i1[:], T.cg[:], False, False, ["i1", "cg"], ["b7"])
+        if not last:
+            mm(P(7), T.in1[:], T.cn[:], False, False, ["in1", "cn"], ["b7"])
         mm(P(3), T.i1[:], T.mask[:], True, False, ["i1", "mask"], ["b3"])
         mm(P(5), T.in1[:], T.mask[:], True, False, ["in1", "mask"], ["b5"])
         mm(P(6), T.in1[:], y, True, False, ["in1", ty], ["b6"])
-        min4(*VCH)
-        min4(*SCH[0])
-        mtok = [max4([VCH])]
-        min4(*SCH[1])
-        mtok.append(max4(SCH[0:1]))
-        min4(*SCH[2])
-        mtok.append(max4(SCH[1:2]))
-        min4(*SCH[3])
-        mtok.append(max4(SCH[2:4]))
-        mall = T.mx[:, 3:4 * B:4]
-        mm(P(6), T.i1[:], mall, False, True, ["i1"] + mtok, ["b6"])
-        act(T.kk2[:], mall, AF.Sign, mtok, ["kk2"])
-        act(zs[:], P(6), AF.Abs, ["b6"], ["zs_%d" % t])
-        send(1, rz[:], zs[:], ["zs_%d" % t], "az_%d" % t)
-        tt(T.kk[:], mall, P(0), GT, mtok + ["b0"], ["kk"])
-        scan(T.ps[:], T.rsw[:], P(4), MIN, MAX, ["rsw", "b4"], ["ps"])
-        pw = T.ps[:, 15:B:16]
-        act(T.t1[:], pw, AF.Identity, ["ps"], ["t1"], bias=M16K)
-        act(T.d1[:, 1:60:6], pw, AF.Identity, ["ps"], ["d1s"], scale=-1.0, bias=-14.5)
-        act(T.d0[:, 1:60:6], T.t1[:], AF.Identity, ["t1"], ["d0s"], scale=1.0 / 512.0, bias=-M16K / 512.0)
+        for what, lo, hi in VCH:
+            if what == "g":
+                cp(T.vv[:, 16 * lo:16 * hi], T.xt[:].indirect(T.st[:, lo:hi]), ["x", "st"], lanes("vv", lo, hi))
+            elif what == "n":
+                scan(T.mn[:, 16 * lo:16 * hi], T.rs1[:, 0:16 * (hi - lo)], T.vv[:, 16 * lo:16 * hi], MAX, MIN,
+                     ["rs1"] + lanes("vv", lo, hi), lanes("mn", lo, hi))
+            else:
+                scan(T.mx[:, 4 * lo:4 * hi], T.rs2[:, 0:4 * (hi - lo)], T.mn[:, 16 * lo + 3:16 * hi:4], MIN, MAX,
+                     ["rs2"] + lanes("mn", lo, hi), lanes("mx", lo, hi))
+        mall, mtok = T.mx[:, 3:4 * B:4], lanes("mx", 0, B)
 
-        def place(j, first):
-            for k, lhs in enumerate(("e15x", "e15", "e15n")):
-                mm(P(j), T[lhs][:], ro[:, B * k:B * k + B], first and k == 0, j != 5 and k == 2, [lhs, "ro_%d" % t], ["b%d" % j])
-        place(3, False)
-        mm(P(7), T.gb[:], T.kk2[:], False, False, ["g8n", "kk2"], ["b7"])
-        mm(P(7), T.g8[:], T.kk[:], False, False, ["g8", "kk"], ["b7"])
-        mm(P(7), T.g1[:], zs[:], False, True, ["g1", "zs_%d" % t], ["b7"])
-        place(2, True)
-        place(6, True)
-        place(5, False)
+        def place(j):
+            mm(P(j), T.e15[:], ro[:], j in (1, 2), j != 5, ["e15", "ro_%d" % t], ["b%d" % j])
+
+        def own():
+            scan(T.dws[:], T.rsw[:], P(3), MIN, MAX, ["rsw", "b3"], ["dws"])
+
+        def named():
+            ts(T.raw[:], T.dws[:, 15:B:16], MID, ADD, ["dws"], ["raw"])
 
         def same(c):
             ts(T.eq[:, c * B + 16 * c:c * B + B], b[2][:, 16 * c:B], T.dws[:, 16 * c - 1:16 * c], EQ, ["b2", "dws"], ["eq%d" % c])
 
         def count(c, src, tok, stop=False):
             mm(b[5][:, 16 * c:B], T.g8[:], src, False, stop, ["g8", tok], ["b5"])
-        scan(T.dws[:], T.rsw[:], P(3), MIN, MAX, ["rsw", "b3"], ["dws"])
-        scan(T.qs[:], T.rsw[:], P(7), MIN, MAX, ["rsw", "b7"], ["qs"])
-        q = T.qs[:, 15:B:16]
+        mm(P(6), T.i1[:], mall, False, True, ["i1"] + mtok, ["b6"])
+        act(T.kk2[:], mall, AF.Sign, mtok, ["kk2"])
+        act(zs[:], P(6), AF.Abs, ["b6"], ["zs_%d" % t])
+        send(1, rz[:], zs[:], ["zs_%d" % t], "az_%d" % t)
+        pw, q = T.ps[:, 15:B:16], T.qs[:, 15:B:16]
         am, tam = T.am[:, t:t + 1], "am%d" % t
-        ts(T.raw[:], T.dws[:, 15:B:16], -OFD, ADD, ["dws"], ["raw"])
-        ts(T.d1[:, 0:60:6], q, -7.0 * 8192.0 - 0.5, GE, ["qs"], ["d1b"], 512.0, ADD)
-        toks = ["d0c", "d0s", "d1c", "d1s", "d1b", "d1x0", "d1x1", "d1x2", "d1x3"]
-        act(T.d1[:, 2:60:6], q, AF.Identity, ["qs", tam], ["d1x0"], bias=am)
+        toks = ["d0c", "d0s", "d1c", "d1s", "d1b", "d1x0", "d1x1", "d1x2", "d1x3", "d1c0", "d1c1", "d1c2"]
+        seg = [sum(B - 16 * k for k in range(1, c + 1)) for c in range(NS + 1)]
+
+        def lines():
+            scan(T.ps[:], T.rsw[:], P(4), MIN, MAX, ["rsw", "b4"], ["ps"])
+
+        def choice():
+            act(T.t1[:], pw, AF.Identity, ["ps"], ["t1"], bias=M16K)
+            act(T.d1[:, 1:60:6], pw, AF.Identity, ["ps"], ["d1s"], scale=-1.0, bias=-14.5)
+            act(T.d0[:, 1:60:6], T.t1[:], AF.Identity, ["t1"], ["d0s"], scale=1.0 / 512.0, bias=-M16K / 512.0)
+
+        def sums():
+            mm(P(7), T.g8[:], T.kk[:], False, False, ["g8", "kk"], ["b7"])
+            mm(P(7), T.g8n[:], T.kk2[:], False, False, ["g8n", "kk2"], ["b7"])
+            mm(P(7), T.g1[:], zs[:], False, True, ["g1", "zs_%d" % t], ["b7"])
+
+        def wrap():
+            scan(T.qs[:], T.rsw[:], P(7), MIN, MAX, ["rsw", "b7"], ["qs"])
+
+        def skip(less):
+            ts(T.d1[:, 0:60:6], q, -7.0 * 8192.0 - less, GE, ["qs"], ["d1b"], 512.0, ADD)
+
+        def program():
+            scan(T.po[:], T.d0[:], T.d1[:], MUL, ADD, toks, ["po"])
+
+        def apart():
+            for c in range(1, NS + 1):
+                act(T.ab[:, seg[c - 1]:seg[c]], b[1][:, 16 * c:B], AF.Abs, ["b1", "dws"], ["ab%d" % c], scale=-1.0,
+                    bias=T.dws[:, 16 * c - 1:16 * c])
+
+        def close():
+            act(T.es[:, 0:seg[NS]], T.ab[:, 0:seg[NS]], AF.Relu, ["ab%d" % c for c in range(1, NS + 1)], ["es"], scale=-1.0, bias=1.0)
+
+        def near():
+            tt(T.eq[:, 1:B], b[2][:, 1:B], T.dws[:, 0:B - 1], EQ, ["b2", "dws"], ["eqd"])
+
+        def counts(first):
+            for c in range(9, NS, -1):
+                if c == first:
+                    mm(b[5][:, 1:B], T.g8[:], T.eq[:, 1:B], False, False, ["g8", "eqd"], ["b5"])
+                if c == NS + (3 if last else EO):
+                    for k in range(1, NS + 1):
+                        count(k, T.es[:, seg[k - 1]:seg[k]], "es")
+                count(c, T.eq[:, c * B + 16 * c:c * B + B], "eq%d" % c, c == NS + 1)
+
+        def target():
+            scan(T.rs[:], T.dumr[:], P(5), MAX, MIN, ["dumr", "b5"], ["rs"])
+
+        def listed():
+            ts(T.dst[:], T.rs[:, 15:B:16], MID, ADD, ["rs"], ["dst"])
+
+        def added():
+            old, tok = (T.wy, WY) if t else (T.ilt, IL)
+            tt(T.ui[:], old[:].indirect(T.raw[:]), rz[:], ADD, tok + ["raw", "rz_%d" % t], ["ui"])
+
+        def turned():
+            ts(T.ui2[:], T.ui[:], 31, AND, ["ui"], ["ui2"])
+
+        tt(T.kk[:], mall, P(0), GT, mtok + ["b0"], ["kk"])
         if not last:
-            act(T.d1[:, 5:60:6], q, AF.Identity, ["qs", tam], ["d1x1"], bias=am)
-            act(T.d1[:, 62:120:6], q, AF.Identity, ["qs", tam], ["d1x2"], bias=am)
+            lines()
+            choice()
+            place(3)
+            sums()
+            for j in (2, 1, 5):
+                place(j)
+            own()
+            wrap()
+            named()
+            skip(32.5)
+            for k, lo in enumerate((2, 5, 62)):
+                act(T.d1[:, lo:lo // 60 * 60 + 60:6], q, AF.Identity, ["qs", tam], ["d1x%d" % k], bias=am)
             ts(T.d1[:, 65:120:6], q, am, ADD, ["qs", tam], ["d1x3"])
             same(9)
-            scan(T.po[:], T.d0[:], T.d1[:], MUL, ADD, toks, ["po"])
+            program()
             same(8)
             ts(m3[:], T.po[:, 5:120:6], 1.0 - OFF, ADD, ["po"], ["m3_%d" % t])
             send(1, T["r3_%d" % t][:], m3[:], ["m3_%d" % t], "a3_%d" % t)
-            mm(b[1][:, 256:266], T.onef[:], T.d1[:, 0:60:6], True, True, ["onef", "d1b"], ["b1"])
-        else:
-            same(9)
-            scan(T.po[:, 0:60], T.d0[:, 0:60], T.d1[:, 0:60], MUL, ADD, toks, ["po"])
-            same(8)
-        seg = [0]
-        for c in range(1, NS + 1):
-            seg.append(seg[-1] + B - 16 * c)
-            act(T.ab[:, seg[c - 1]:seg[c]], b[6][:, 16 * c:B], AF.Abs, ["b6", "dws"], ["ab%d" % c], scale=-1.0, bias=T.dws[:, 16 * c - 1:16 * c])
-        act(T.es[:, 0:seg[NS]], T.ab[:, 0:seg[NS]], AF.Relu, ["ab%d" % c for c in range(1, NS + 1)], ["es"], scale=-1.0, bias=1.0)
-        tt(T.eq[:, 1:B], b[2][:, 1:B], T.dws[:, 0:B - 1], EQ, ["b2", "dws"], ["eqd"])
-        for c in range(7, NS, -1):
-            same(c)
-        for c in range(9, NS, -1):
-            count(c, T.eq[:, c * B + 16 * c:c * B + B], "eq%d" % c)
-            if c == 8:
-                mm(b[5][:, 1:B], T.g8[:], T.eq[:, 1:B], False, False, ["g8", "eqd"], ["b5"])
-        for c in range(1, NS + 1):
-            count(c, T.es[:, seg[c - 1]:seg[c]], "es", c == NS)
-        act(hs[:, 0:10], q, AF.Identity, ["qs"], ["hsa_%d" % (t + 1)], bias=-float(t))
-        act(hs[:, 10:20], T.d1[:, 2:60:6], AF.Identity, ["d1x0"], ["hsb_%d" % (t + 1)], bias=-float(t))
-        if last:
-            act(hs[:, 20:30], T.po[:, 1:60:6], AF.Identity, ["po"], ["hsc"], scale=-0.03125, bias=-136.0 - 14.5 / 32.0)
-            send(1, T.hb[:, 80:110], hs[:], ["hsa_4", "hsb_4", "hsc"], "ah_4")
-        else:
-            act(T.junk[:], b[1][:, 256:266], AF.Identity, ["b1"], ["junk", "am%d" % (t + 1)], bias=-65536.0, accum_out=T.am[:, t + 1:t + 2])
+            if t == 0:
+                narrow(4)
+            apart()
+            close()
+            near()
+            for c in range(7, NS, -1):
+                same(c)
+            counts(7)
+            mm(b[4][:, 256:266], T.onef[:], T.d1[:, 0:60:6], True, True, ["onef", "d1b"], ["b4"])
+            act(hs[:, 0:10], q, AF.Identity, ["qs"], ["hsa_%d" % (t + 1)], bias=-float(t))
+            act(hs[:, 10:20], T.d1[:, 2:60:6], AF.Identity, ["d1x0"], ["hsb_%d" % (t + 1)], bias=-float(t))
+            act(T.junk[:], b[4][:, 256:266], AF.Identity, ["b4"], ["junk", "am%d" % (t + 1)], bias=-65536.0, accum_out=T.am[:, t + 1:t + 2])
             twice(rz[:], "rz_%d" % t)
-        tt(T.ui[:], T.wy[:].indirect(T.raw[:]), rz[:], ADD, WY + ["raw", "rz_%d" % t], ["ui"])
-        scan(T.rs[:], T.dumr[:], P(5), MAX, MIN, ["dumr", "b5"], ["rs"])
-        ts(T.ui2[:], T.ui[:], 31, AND, ["ui"], ["ui2"])
-        ts(T.dst[:], T.rs[:, 15:B:16], -OFD, ADD, ["rs"], ["dst"])
+            added()
+            target()
+            turned()
+            listed()
+        else:
+            for j in (3, 1, 2, 5):
+                place(j)
+            sums()
+            lines()
+            own()
+            apart()
+            near()
+            named()
+            close()
+            choice()
+            for c in range(9, NS, -1):
+                same(c)
+                if c == LP:
+                    wrap()
+                if c == LP - 1:
+                    skip(0.5)
+            for k, lo in ((2, 62), (3, 65)):
+                act(T.d1[:, lo:120:6], q, AF.Copy, ["qs"], ["d1x%d" % k])
+            counts(9)
+            program()
+            act(hs[:, 0:10], T.po[:, 1:60:6], AF.Identity, ["po"], ["hsa_4"], scale=-0.03125, bias=-136.0 - 14.5 / 32.0)
+            act(hs[:, 10:20], T.po[:, 65:120:6], AF.Identity, ["po", "am7"], ["hsb_4"], bias=T.am[:, 7:8])
+            send(1, T.hb[:, 80:100], hs[:], ["hsa_4", "hsb_4"], "ah_4")
+            tt(T.fa[:], T.hb[:, 20:80], T.hb[:, 10:70], SUB, HB[0:RO], ["fa"])
+            target()
+            added()
+            listed()
+            turned()
+            ts(T.fb[:], T.fa[:], 31, AND, ["fa"], ["fb"])
         cp(T.wy[:].indirect(T.dst[:]), T.ui2[:], ["ui2", "dst"], WY)
+    cp(T.fc[:], T.fb[:], ["fb"], ["fc"])
+    dma("Y", T.yy[:], T["rz_3"][:], ["rz_3"], [], "oyy")
     dma("Y", T.yw[:], T.wy[:, 0:W], WY, [], "oyw")
-    dma("S", T.yy[:], T["rz_3"][:], ["rz_3"], [], "oyy")
-    HB = ["hb%d" % t for t in range(RO + 1)]
-    for t in range(RO + 1):
-        arrives(RO - max(t - 1, 0), HB[t], "ah_%d" % t)
-    tt(T.fa[:], T.hb[:, 20:100], T.hb[:, 10:90], SUB, HB, ["fa"])
-    ts(T.fb[:], T.fa[:], 31, AND, ["fa"], ["fb"])
-    tt(T.fc[:], T.fb[:, 0:40], T.fb[:, 40:80], ADD, ["fb"], ["fc"])
-    tt(T.fd[:], T.fc[:, 0:20], T.fc[:, 20:40], ADD, ["fc"], ["fd"])
-    tt(T.fe[:], T.fd[:, 0:10], T.hb[:, 0:10], ADD, ["fd"], ["fe"])
-    tt(T.ff[:], T.fd[:, 10:20], T.fe[:], ADD, ["fd", "fe"], ["ff"])
-    ts(T.fg[:], T.ff[:], 4095, AND, ["ff"], ["fg"])
-    cp(T.hb[:, 110:120], T.fg[:], ["fg"], ["hbt"])
-    for p in range(16):
-        mm(b[1][0:8, p:2 * B:16], T.idf[:, p:128:16], T.hb[:, 100:120], True, True, ["idf", "hbt"] + HB, ["b1"])
-    cp(T.fin[:], b[1][0:8, 0:2 * B], ["b1"], ["fin"])
-    dma("S", T.yl[:], T.fin[:, 0:B], ["fin"], [], "osm")
-    dma("Y", T.yt[:], T.fin[:, B:2 * B], ["fin"], [], "osn")
+
+    def unwrap(j, src, toks):
+        for p in range(16):
+            mm(b[j][0:8, p:B:16], T.idf[:, p:128:16], src, True, True, ["idf"] + toks, ["b%d" % j])
+    mm(b[3][:, 0:10], T.idf[:], T.hb[:, 0:10], True, False, ["idf", "hb0"], ["b3"])
+    for k in range(6):
+        mm(b[3][:, 0:10], T.i1[:], T.fc[:, 10 * k:10 * k + 10], False, k == 5, ["i1", "fc"], ["b3"])
+    unwrap(4, T.hb[:, 80:90], ["hb4"])
+    act(T.fl[:], b[4][0:8, 0:B], AF.Copy, ["b4"], ["fl"])
+    dma("S", T.yl[:], T.fl[:], ["fl"], [], "osm")
+    tt(T.fh[:], b[3][:, 0:10], T.hb[:, 90:100], ADD, ["b3", "hb4"], ["fh"])
+    ts(T.fi[:], T.fh[:], 4095, AND, ["fh"], ["fi"])
+    cp(T.hb[:, 100:110], T.fi[:], ["fi"], ["hbt"])
+    unwrap(6, T.hb[:, 100:110], ["hbt"])
+    cp(T.ft[:], b[6][0:8, 0:B], ["b6"], ["ft"])
+    dma("Y", T.yt[:], T.ft[:], ["ft"], [], "osn")
     g.wait_ge(T.sem.loc, sent[0])
     for s, v in tot.items():
         if know["P"].get(s, 0) < v:

from concourse.mybir import AluOpType, ActivationFunctionType

W, B, RO = 3712, 160, 4
PIECES = [(0, 1856), (1856, W)]
UNITS = [(0, 928), (928, 1856), (1856, 2464), (2464, 3072), (3072, W)]
SCH = [(48, 92), (92, 130), (130, 152), (152, 160)]
VCH = [("g", 0, 24), ("g", 24, 48), ("n", 0, 24), ("n", 48, 92), ("n", 24, 48), ("n", 92, 130), ("x", 0, 92), ("n", 130, 152),
       ("x", 92, 130), ("n", 152, 160), ("x", 130, 160)]
OFF = 4352.0
OFS = OFF - 32.0
MID = 1856.0
NF, NL = 2, 2
WV = False
EO = 2
LP = 6
M32 = 402653184.0
M16 = 201326592.0
M16K = 1.5 * 2.0 ** 37

F32, BF, F16, I32, U16 = "float32", "bfloat16", "float16", "int32", "uint16"
SCRATCH = {}
for _dt, _rows, _list in (
    (I32, 128, {"ilt": W, "tmp": W, "wgi": B, "ui": B, "ui2": B, "pq": B, "pq2": B, "pm0": 10, "pm": 10, "c16": 10,
                "fa": 60, "fb": 60, "fh": 10, "fi": 10}),
    (BF, 128, {"xt": W, "wy": W + B, "colt": W, "vv": 16 * B, "mn": 16 * B, "mx": 4 * B, "eq": 10 * B, "y0t": B, "kk": B, "kk2": B,
               "lg": B, "wg": B, "cn": B, "cy": B, "ones": B, "g1": 128, "g8n": 128, "i1": 128, "i32": 128, "in1": 128, "in32": 128, "g8": 128,
               "eb": 128, "e0x": 128, "e1x": 128, "jr": 128, "ja": 128, "mask": B, "ab": 6 * B, "es": 6 * B, "rs1": 768, "rs2": 384, "fc": 60}),
    (F32, 128, {"dws": B, "ps": B, "rs": B, "qs": B, "q16": B, "rsw": B, "dumr": B, "d0": 120, "d1": 120, "po": 120, "t1": 10, "li": 10,
                "am": 8, "junk": 10, "onef": 128, "idf": 128, "hb": 110}),
    (F16, 128, {"e15": 128}),
    (U16, 128, {"st": B, "aw0": 10, "raw": 10, "dst": 10}),
    (I32, 8, {"ln8": B, "tk8": B, "ti8": B, "th8": B}),
    (BF, 8, {"lb8": B, "tb8": B, "tc8": B, "sel": 128, "sel32": 128}),
    (F32, 8, {"fl": B, "ft": B}),
):
    for _k, _n in _list.items():
        SCRATCH[_k] = ("sbuf", [_rows, _n], _dt)
for _t in range(RO):
    for _k in ("op", "ro"):
        SCRATCH["%s_%d" % (_k, _t)] = ("sbuf", [128, B], F16)
    for _k in ("zs", "rz"):
        SCRATCH["%s_%d" % (_k, _t)] = ("sbuf", [128, B], BF)
    for _k in ("m3", "r3"):
        SCRATCH["%s_%d" % (_k, _t)] = ("sbuf", [128, 20], U16)
for _t in range(RO + 1):
    SCRATCH["hs_%d" % _t] = ("sbuf", [128, 20], F32)
for _t in range(8):
    SCRATCH["b%d" % _t] = ("psum", [128, 512], F32)
SEMAPHORES = ["qV", "qS", "qT", "qP", "loc", "dil0", "dil1", "dx", "dy", "dln", "dtk", "oyy", "oyw", "osm", "osn"]
SEMAPHORES += ["a%s_%d" % (m, t) for m in ("o", "z", "3") for t in range(RO)] + ["ah_%d" % t for t in range(RO + 1)]


def rank_program(g, core, T, topo):
    rank = T.rank_of(core)
    if rank is None:
        return
    n = len(T.cores)
    OP, AF = AluOpType, ActivationFunctionType
    ADD, SUB, MUL, MAX, MIN, EQ, GE, GT, LT = OP.add, OP.subtract, OP.mult, OP.max, OP.min, OP.is_equal, OP.is_ge, OP.is_gt, OP.is_lt
    AND, SHR = OP.bitwise_and, OP.arith_shift_right
    eng = {"V": g.vector, "S": g.scalar, "T": g.tensor, "P": g, "Y": g.sync}
    know = {e: {} for e in eng}
    tot, lastw, readers = {}, {}, {}

    def waits(e, r, w):
        deps = []
        for k in r:
            deps += lastw.get(k, [])
        for k in w:
            deps += lastw.get(k, []) + readers.get(k, [])
        deps = [d for d in deps if know[e].get(d[0], 0) < d[1] and not (e == "T" and d[0] == "qT")]
        need = {}
        for d in deps:
            if d[0] not in need or need[d[0]][1] < d[1]:
                need[d[0]] = d
        keep = [d for d in need.values() if not any(o is not d and o[2].get(d[0], 0) >= d[1] for o in need.values())]
        for d in keep:
            eng[e].wait_ge(T.sem[d[0]], d[1])
        for d in need.values():
            for s, v in list(d[2].items()) + [(d[0], d[1])]:
                know[e][s] = max(know[e].get(s, 0), v)

    def done(e, inst, r, w, sem, inc):
        tot[sem] = tot.get(sem, 0) + inc
        inst.then_inc(T.sem[sem], inc)
        snap = dict(know[e])
        snap[sem] = tot[sem]
        ev = (sem, tot[sem], snap)
        for k in r:
            readers.setdefault(k, []).append(ev)
        for k in w:
            lastw[k] = [ev]
            readers[k] = []

    def do(e, fn, r, w):
        waits(e, r, w)
        done(e, fn(eng[e]), r, w, "q" + e, 1)

    def dma(e, out, in_, r, w, sem):
        waits(e, r, w)
        done(e, eng[e].dma_start(out, in_), r, w, sem, 16)

    def tt(out, a, b, op, r, w):
        do("V", lambda v: v.tensor_tensor(out, a, b, op), r, w)

    def ts(out, a, s1, o1, r, w, s2=None, o2=None):
        if o2 is None:
            do("V", lambda v: v.tensor_scalar(out, a, s1, None, o1), r, w)
        else:
            do("V", lambda v: v.tensor_scalar(out, a, s1, s2, o1, o2), r, w)

    def cp(out, a, r, w):
        do("V", lambda v: v.tensor_copy(out, a), r, w)

    def ms(ap, val, w):
        do("V", lambda v: v.memset(ap, val), [], [w])

    def scan(out, x0, x1, o0, o1, r, w):
        do("V", lambda v: v.tensor_tensor_scan(out, x0, x1, 0.0, o0, o1), r, w)

    def mm(out, lhs, rhs, start, stop, r, w):
        do("T", lambda v: v.matmul(out, lhs, rhs, start, stop), r, w)

    def act(out, in_, func, r, w, **kw):
        do("S", lambda v: v.activation(out, in_, func, **kw), r, w)

    def pool(fn, r, w):
        do("P", fn, r, w)

    sent = [0]

    def send(hops, out, in_, r, sem):
        waits("P", r, [])
        to = T.cores[(rank + hops) % n]
        rid, pid, _se = topo.addr(to)
        g.remote_dma(out, in_, T.sem[sem], T.sem.loc, pid, rid, topo.mask(core, to))
        sent[0] += len(topo.engines(core, to))

    def arrives(hops, tok, sem):
        na = len(topo.engines(T.cores[(rank - hops) % n], core))
        lastw[tok] = [(sem, na, {sem: na})]
        tot[sem] = na

    b = [T["b%d" % j] for j in range(8)]
    P = lambda j: b[j][:, 0:B]

    dma("Y", T.ln8[:], T.ln0[:], [], ["ln8"], "dln")
    dma("S", T.tk8[:], T.tk0[:], [], ["tk8"], "dtk")
    for q, (lo, hi) in enumerate(PIECES):
        dma("Y", T.ilt[:, lo:hi], T.il[:, lo:hi], [], ["il%d" % q], "dil%d" % q)
    dma("Y", T.xt[:], T.xw[:], [], ["x"], "dx")
    dma("Y", T.y0t[:], T.y0[:], [], ["y0"], "dy")

    small = {"allow_small_or_imprecise_dtypes": True}
    ms(T.ones[:], 1.0, "ones")
    pool(lambda p: p.iota(T.pq[:], [[0, 10], [1, 16]], 128, -1), [], ["pq"])
    pool(lambda p: p.iota(T.q16[:], [[0, 10], [1, 16]], 0, 0, **small), [], ["q16"])
    pool(lambda p: p.affine_select(T.i1[:], T.ones[:, 0:128], [[-1, 128]], EQ, 0.0, 0, 1), ["ones"], ["i1"])
    pool(lambda p: p.affine_select(T.sel[:], T.ones[0:8, 0:128], [[1, 8], [0, 16]], EQ, 0.0, 0, -1), ["ones"], ["sel"])
    pool(lambda p: p.iota(T.colt[:, 0:928], [[0, 29], [-1, 32]], 32, 0, **small), [], ["colt0"])
    pool(lambda p: p.iota(T.jr[:], [[-16, 8], [0, 16]], 0, 1, **small), [], ["jr"])
    pool(lambda p: p.iota(T.pm0[:], [[0, 10]], 0, 1), [], ["pm0"])
    pool(lambda p: p.iota(T.c16[:], [[16, 10]], 0, 0), [], ["c16"])
    CT = ["colt%d" % j for j in range(4)]

    def fill(ap, n_, v, w):
        act(ap, T.ones[:, 0:n_], AF.Copy, ["ones"], [w], scale=v)
    fill(T.d0[:], 120, 1.0, "d0c")
    fill(T.d1[:], 120, 0.0, "d1c")
    fill(T.dumr[:], B, -4096.0, "dumr")
    for lo, v in ((0, 0.0), (5, -1.0)):
        fill(T.d0[:, lo:120:6], 20, v, "d0c")
    for lo, hi, v in ((3, 60, M32), (4, 60, -M32), (63, 120, M16), (64, 120, -M16)):
        fill(T.d1[:, lo:hi:6], 10, v, "d1c")
    for k in ("d1b", "d1s", "d1x0", "d1x1", "d1x2", "d1x3"):
        lastw[k] = lastw["d1c"]
    lastw["d0s"] = lastw["d0c"]
    fill(T.am[:, 0:1], 1, 0.0, "am0")
    fill(T.onef[:], 128, 1.0, "onef")
    fill(T.wy[:, W:W + B], B, 0.0, "wyd")
    ms(T.rs1[:], 0.0, "rs1")
    ms(T.rs2[:], 512.0, "rs2")
    ms(T.rs1[:, 0:768:4], 512.0, "rs1")
    ms(T.rs2[:, 0:384:4], 0.0, "rs2")

    ts(T.pq2[:], T.pq[:], 15, AND, ["pq"], ["pq2"])
    ts(T.rsw[:], T.q16[:], -0.5, ADD, ["q16"], ["rsw"], 1e27, MUL)
    ts(T.mask[:], T.pq2[:], 0.0, GT, ["pq2"], ["mask"], -(2.0 ** 60), MUL)
    act(T.sel32[:], T.sel[:], AF.Copy, ["sel"], ["sel32"], scale=32.0)
    cp(T.lb8[:], T.ln8[:], ["ln8"], ["lb8"])
    ts(T.ti8[:], T.tk8[:], 31, AND, ["tk8"], ["ti8"])
    ts(T.th8[:], T.tk8[:], 5, SHR, ["tk8"], ["th8"])
    cp(T.tb8[:], T.ti8[:], ["ti8"], ["tb8"])
    cp(T.tc8[:], T.th8[:], ["th8"], ["tc8"])
    for j, hi in ((0, "lb8"), (1, "tc8")):
        mm(P(j), T.i1[:], T.mask[:], True, False, ["i1", "mask"], ["b%d" % j])
        mm(P(j), T.sel32[:], T[hi][:], False, False, ["sel32", hi], ["b%d" % j])
        mm(P(j), T.sel[:], T.tb8[:], False, True, ["sel", "tb8"], ["b%d" % j])
    scan(T.qs[:], T.rsw[:], P(0), MIN, MAX, ["rsw", "b0"], ["qs"])
    scan(T.ps[:], T.rsw[:], P(1), MIN, MAX, ["rsw", "b1"], ["ps"])
    cp(T.aw0[:], T.qs[:, 15:B:16], ["qs"], ["aw_0"])
    for k, v in (("i32", 32.0), ("in1", -1.0), ("in32", -32.0), ("idf", 1.0)):
        act(T[k][:], T.i1[:], AF.Copy, ["i1"], [k], scale=v)
    act(T.hs_0[:, 0:10], T.ps[:, 15:B:16], AF.Identity, ["ps"], ["hsa_0"], bias=float(RO))
    act(T.hs_0[:, 10:20], T.ps[:, 15:B:16], AF.Copy, ["ps"], ["hsb_0"])
    send(RO, T.hb[:, 0:20], T.hs_0[:, 0:20], ["hsa_0", "hsb_0"], "ah_0")
    act(T.ja[:], T.jr[:], AF.Abs, ["jr"], ["ja"], bias=-7.5)
    for j in range(1, 4):
        act(T.colt[:, 928 * j:928 * j + 928], T.colt[:, 0:928], AF.Copy, ["colt0"], ["colt%d" % j])

    for k, row, v in (("e15", 15.0, 1.0), ("eb", 0.0, 32.0), ("e0x", 0.0, 16384.0), ("e1x", 1.0, -16384.0)):
        ts(T[k][:], T.jr[:], row, EQ, ["jr"], [k], v, MUL)
    ts(T.pm[:], T.pm0[:], 15, AND, ["pm0"], ["pm"])
    for k, v in (("g1", 1.0), ("g8", 8192.0), ("g8n", -8192.0)):
        ts(T[k][:], T.ja[:], 8.0, LT, ["ja"], [k], v, MUL)
    tt(T.li[:], T.pm[:], T.c16[:], ADD, ["pm", "c16"], ["li"])
    act(T.d1[:, 60:120:6], T.li[:], AF.Identity, ["li"], ["d1c"], bias=-OFF - 6.5, scale=-16.0)
    act(T.dumr[:, 0:B:16], T.li[:], AF.Identity, ["li"], ["dumr"], bias=W - MID)

    WY = ["wy%d" % u for u in range(len(UNITS))] + ["wyd"]
    IL = ["il0", "il1"]

    def low5(u):
        lo, hi = UNITS[u]
        ts(T.tmp[:, lo:hi], T.ilt[:, lo:hi], 31, AND, ["il%d" % (lo >= PIECES[1][0])], ["tmp%d" % u])

    def narrow(u):
        lo, hi = UNITS[u]
        pool(lambda p: p.affine_select(T.wy[:, lo:hi], T.tmp[:, lo:hi], [[0, hi - lo]], GE, 0.0, 0, 0), ["tmp%d" % u], ["wy%d" % u])

    for u in range(2):
        low5(u)
        narrow(u)

    def twice(y, ty):
        act(P(0), y, AF.Relu, [ty], ["b0"], scale=2.0, bias=-1.0)

    def lanes(k, lo, hi):
        return ["%s%d" % (k, i) for i in range(lo, hi, 2)]

    HB = ["hb%d" % t for t in range(RO + 1)]
    for t in range(RO + 1):
        arrives(RO - max(t - 1, 0), HB[t], "ah_%d" % t)

    for t in range(RO):
        last = t == RO - 1
        NS = NL if last else NF
        op, zs, m3, ro, rz = (T[k % t] for k in ("op_%d", "zs_%d", "m3_%d", "ro_%d", "rz_%d"))
        hs = T["hs_%d" % (t + 1)]
        if t == 0:
            y, ty, aw, taw = T.y0t[:], "y0", T.aw0[:], "aw_0"
        else:
            y, ty = T["rz_%d" % (t - 1)][:], "rz_%d" % (t - 1)
            aw, taw = T["r3_%d" % (t - 1)][:, 0:10], "r3_%d" % (t - 1)
        arrives(1, "ro_%d" % t, "ao_%d" % t)
        arrives(1, "rz_%d" % t, "az_%d" % t)
        if not last:
            arrives(1, "r3_%d" % t, "a3_%d" % t)

        def words():
            cp(T.xt[:, 0:16 * B].indirect(T["r3_%d" % (t - 1)][:, 10:20]), y, [ty, taw], ["x"])
        act(T.cn[:], T.colt[:].indirect(aw), AF.Copy, CT + [taw], ["cn"])
        act(T.lg[:], T.ilt[:].indirect(aw), AF.Identity, IL + [taw], ["lg"], scale=0.03125, bias=136.0 - 31.0 / 64.0)
        if t and not WV:
            act(T.wg[:], T.wy[:].indirect(aw), AF.Copy, WY + [taw], ["wg"])
        if t == 0:
            ts(T.wgi[:], T.ilt[:].indirect(aw), 31, AND, IL + [taw], ["wgi"])
            low5(2)
            cp(T.wg[:], T.wgi[:], ["wgi"], ["wg"])
            tt(T.cy[:], T.wgi[:], T.cn[:], GE, ["wgi", "cn"], ["cy"])
            low5(3)
        elif WV:
            cp(T.wg[:], T.wy[:].indirect(aw), WY + [taw], ["wg"])
            tt(T.cy[:], T.wg[:], T.cn[:], GE, ["wg", "cn"], ["cy"])
            words()
        else:
            tt(T.cy[:], T.wy[:].indirect(aw), T.cn[:], GE, WY + [taw, "cn"], ["cy"])
            words()
        for k, (lhs, rhs) in enumerate((("in1", "cn"), ("i32", "lg"), ("i1", "wg"), ("in32", "cy"))):
            mm(P(1), T[lhs][:], T[rhs][:], k == 0, k == 3, [lhs, rhs], ["b1"])
        ts(T.st[:], P(1), -OFS, ADD, ["b1"], ["st"])
        ts(op[:], P(1), -OFS - MID, ADD, ["b1"], ["op"])
        send(1, ro[:], op[:], ["op"], "ao_%d" % t)
        if t:
            send(RO - t + 1, T.hb[:, 20 * t:20 * t + 20], T["hs_%d" % t][:], ["hsa_%d" % t, "hsb_%d" % t], "ah_%d" % t)
        else:
            low5(4)
            narrow(2)
            narrow(3)
        for lo, hi in SCH:
            act(T.vv[:, 16 * lo:16 * hi], T.xt[:].indirect(T.st[:, lo:hi]), AF.Copy, ["x", "st"], lanes("vv", lo, hi))
        if t == 0:
            twice(y, ty)
        if last:
            for k, (lo, v) in enumerate(((60, -15.5), (63, M32), (64, -M32))):
                act(T.am[:, 4 + k:5 + k], T.am[:, 3 + k:4 + k], AF.Identity, ["am%d" % (3 + k)], ["am%d" % (4 + k)], bias=v)
                act(T.d1[:, lo:120:6], T.ones[:, 0:10], AF.Copy, ["ones", "po"], ["d1c%d" % k], scale=v)
            act(T.am[:, 7:8], T.am[:, 6:7], AF.Identity, ["am6", "am3"], ["am7"], scale=-1.0, bias=T.am[:, 3:4])
        mm(P(4), T.i1[:], T.mask[:], True, False, ["i1", "mask"], ["b4"])
        for k in ("e0x", "e1x", "eb"):
            mm(P(4), T[k][:], T.lg[:], False, k == "eb", [k, "lg"], ["b4"])
        mm(P(7), T.i1[:], T.mask[:], True, False, ["i1", "mask"], ["b7"])
        if not last:
            mm(P(7), T.in1[:], T.cn[:], False, False, ["in1", "cn"], ["b7"])
        mm(P(3), T.i1[:], T.mask[:], True, False, ["i1", "mask"], ["b3"])
        mm(P(5), T.in1[:], T.mask[:], True, False, ["in1", "mask"], ["b5"])
        mm(P(6), T.in1[:], y, True, False, ["in1", ty], ["b6"])
        for what, lo, hi in VCH:
            if what == "g":
                cp(T.vv[:, 16 * lo:16 * hi], T.xt[:].indirect(T.st[:, lo:hi]), ["x", "st"], lanes("vv", lo, hi))
            elif what == "n":
                scan(T.mn[:, 16 * lo:16 * hi], T.rs1[:, 0:16 * (hi - lo)], T.vv[:, 16 * lo:16 * hi], MAX, MIN,
                     ["rs1"] + lanes("vv", lo, hi), lanes("mn", lo, hi))
            else:
                scan(T.mx[:, 4 * lo:4 * hi], T.rs2[:, 0:4 * (hi - lo)], T.mn[:, 16 * lo + 3:16 * hi:4], MIN, MAX,
                     ["rs2"] + lanes("mn", lo, hi), lanes("mx", lo, hi))
        mall, mtok = T.mx[:, 3:4 * B:4], lanes("mx", 0, B)

        def place(j):
            mm(P(j), T.e15[:], ro[:], j in (1, 2), j != 5, ["e15", "ro_%d" % t], ["b%d" % j])

        def own():
            scan(T.dws[:], T.rsw[:], P(3), MIN, MAX, ["rsw", "b3"], ["dws"])

        def named():
            ts(T.raw[:], T.dws[:, 15:B:16], MID, ADD, ["dws"], ["raw"])

        def same(c):
            ts(T.eq[:, c * B + 16 * c:c * B + B], b[2][:, 16 * c:B], T.dws[:, 16 * c - 1:16 * c], EQ, ["b2", "dws"], ["eq%d" % c])

        def count(c, src, tok, stop=False):
            mm(b[5][:, 16 * c:B], T.g8[:], src, False, stop, ["g8", tok], ["b5"])
        mm(P(6), T.i1[:], mall, False, True, ["i1"] + mtok, ["b6"])
        act(T.kk2[:], mall, AF.Sign, mtok, ["kk2"])
        act(zs[:], P(6), AF.Abs, ["b6"], ["zs_%d" % t])
        send(1, rz[:], zs[:], ["zs_%d" % t], "az_%d" % t)
        pw, q = T.ps[:, 15:B:16], T.qs[:, 15:B:16]
        am, tam = T.am[:, t:t + 1], "am%d" % t
        toks = ["d0c", "d0s", "d1c", "d1s", "d1b", "d1x0", "d1x1", "d1x2", "d1x3", "d1c0", "d1c1", "d1c2"]
        seg = [sum(B - 16 * k for k in range(1, c + 1)) for c in range(NS + 1)]

        def lines():
            scan(T.ps[:], T.rsw[:], P(4), MIN, MAX, ["rsw", "b4"], ["ps"])

        def choice():
            act(T.t1[:], pw, AF.Identity, ["ps"], ["t1"], bias=M16K)
            act(T.d1[:, 1:60:6], pw, AF.Identity, ["ps"], ["d1s"], scale=-1.0, bias=-14.5)
            act(T.d0[:, 1:60:6], T.t1[:], AF.Identity, ["t1"], ["d0s"], scale=1.0 / 512.0, bias=-M16K / 512.0)

        def sums():
            mm(P(7), T.g8[:], T.kk[:], False, False, ["g8", "kk"], ["b7"])
            mm(P(7), T.g8n[:], T.kk2[:], False, False, ["g8n", "kk2"], ["b7"])
            mm(P(7), T.g1[:], zs[:], False, True, ["g1", "zs_%d" % t], ["b7"])

        def wrap():
            scan(T.qs[:], T.rsw[:], P(7), MIN, MAX, ["rsw", "b7"], ["qs"])

        def skip(less):
            ts(T.d1[:, 0:60:6], q, -7.0 * 8192.0 - less, GE, ["qs"], ["d1b"], 512.0, ADD)

        def program():
            scan(T.po[:], T.d0[:], T.d1[:], MUL, ADD, toks, ["po"])

        def apart():
            for c in range(1, NS + 1):
                act(T.ab[:, seg[c - 1]:seg[c]], b[1][:, 16 * c:B], AF.Abs, ["b1", "dws"], ["ab%d" % c], scale=-1.0,
                    bias=T.dws[:, 16 * c - 1:16 * c])

        def close():
            act(T.es[:, 0:seg[NS]], T.ab[:, 0:seg[NS]], AF.Relu, ["ab%d" % c for c in range(1, NS + 1)], ["es"], scale=-1.0, bias=1.0)

        def near():
            tt(T.eq[:, 1:B], b[2][:, 1:B], T.dws[:, 0:B - 1], EQ, ["b2", "dws"], ["eqd"])

        def counts(first):
            for c in range(9, NS, -1):
                if c == first:
                    mm(b[5][:, 1:B], T.g8[:], T.eq[:, 1:B], False, False, ["g8", "eqd"], ["b5"])
                if c == NS + (3 if last else EO):
                    for k in range(1, NS + 1):
                        count(k, T.es[:, seg[k - 1]:seg[k]], "es")
                count(c, T.eq[:, c * B + 16 * c:c * B + B], "eq%d" % c, c == NS + 1)

        def target():
            scan(T.rs[:], T.dumr[:], P(5), MAX, MIN, ["dumr", "b5"], ["rs"])

        def listed():
            ts(T.dst[:], T.rs[:, 15:B:16], MID, ADD, ["rs"], ["dst"])

        def added():
            old, tok = (T.wy, WY) if t else (T.ilt, IL)
            tt(T.ui[:], old[:].indirect(T.raw[:]), rz[:], ADD, tok + ["raw", "rz_%d" % t], ["ui"])

        def turned():
            ts(T.ui2[:], T.ui[:], 31, AND, ["ui"], ["ui2"])

        tt(T.kk[:], mall, P(0), GT, mtok + ["b0"], ["kk"])
        if not last:
            lines()
            choice()
            place(3)
            sums()
            for j in (2, 1, 5):
                place(j)
            own()
            wrap()
            named()
            skip(32.5)
            for k, lo in enumerate((2, 5, 62)):
                act(T.d1[:, lo:lo // 60 * 60 + 60:6], q, AF.Identity, ["qs", tam], ["d1x%d" % k], bias=am)
            ts(T.d1[:, 65:120:6], q, am, ADD, ["qs", tam], ["d1x3"])
            same(9)
            program()
            same(8)
            ts(m3[:], T.po[:, 5:120:6], 1.0 - OFF, ADD, ["po"], ["m3_%d" % t])
            send(1, T["r3_%d" % t][:], m3[:], ["m3_%d" % t], "a3_%d" % t)
            if t == 0:
                narrow(4)
            apart()
            close()
            near()
            for c in range(7, NS, -1):
                same(c)
            counts(7)
            mm(b[4][:, 256:266], T.onef[:], T.d1[:, 0:60:6], True, True, ["onef", "d1b"], ["b4"])
            act(hs[:, 0:10], q, AF.Identity, ["qs"], ["hsa_%d" % (t + 1)], bias=-float(t))
            act(hs[:, 10:20], T.d1[:, 2:60:6], AF.Identity, ["d1x0"], ["hsb_%d" % (t + 1)], bias=-float(t))
            act(T.junk[:], b[4][:, 256:266], AF.Identity, ["b4"], ["junk", "am%d" % (t + 1)], bias=-65536.0, accum_out=T.am[:, t + 1:t + 2])
            twice(rz[:], "rz_%d" % t)
            added()
            target()
            turned()
            listed()
        else:
            for j in (3, 1, 2, 5):
                place(j)
            sums()
            lines()
            own()
            apart()
            near()
            named()
            close()
            choice()
            for c in range(9, NS, -1):
                same(c)
                if c == LP:
                    wrap()
                if c == LP - 1:
                    skip(0.5)
            for k, lo in ((2, 62), (3, 65)):
                act(T.d1[:, lo:120:6], q, AF.Copy, ["qs"], ["d1x%d" % k])
            counts(9)
            program()
            act(hs[:, 0:10], T.po[:, 1:60:6], AF.Identity, ["po"], ["hsa_4"], scale=-0.03125, bias=-136.0 - 14.5 / 32.0)
            act(hs[:, 10:20], T.po[:, 65:120:6], AF.Identity, ["po", "am7"], ["hsb_4"], bias=T.am[:, 7:8])
            send(1, T.hb[:, 80:100], hs[:], ["hsa_4", "hsb_4"], "ah_4")
            tt(T.fa[:], T.hb[:, 20:80], T.hb[:, 10:70], SUB, HB[0:RO], ["fa"])
            target()
            added()
            listed()
            turned()
            ts(T.fb[:], T.fa[:], 31, AND, ["fa"], ["fb"])
        cp(T.wy[:].indirect(T.dst[:]), T.ui2[:], ["ui2", "dst"], WY)
    cp(T.fc[:], T.fb[:], ["fb"], ["fc"])
    dma("Y", T.yy[:], T["rz_3"][:], ["rz_3"], [], "oyy")
    dma("Y", T.yw[:], T.wy[:, 0:W], WY, [], "oyw")

    def unwrap(j, src, toks):
        for p in range(16):
            mm(b[j][0:8, p:B:16], T.idf[:, p:128:16], src, True, True, ["idf"] + toks, ["b%d" % j])
    mm(b[3][:, 0:10], T.idf[:], T.hb[:, 0:10], True, False, ["idf", "hb0"], ["b3"])
    for k in range(6):
        mm(b[3][:, 0:10], T.i1[:], T.fc[:, 10 * k:10 * k + 10], False, k == 5, ["i1", "fc"], ["b3"])
    unwrap(4, T.hb[:, 80:90], ["hb4"])
    act(T.fl[:], b[4][0:8, 0:B], AF.Copy, ["b4"], ["fl"])
    dma("S", T.yl[:], T.fl[:], ["fl"], [], "osm")
    tt(T.fh[:], b[3][:, 0:10], T.hb[:, 90:100], ADD, ["b3", "hb4"], ["fh"])
    ts(T.fi[:], T.fh[:], 4095, AND, ["fh"], ["fi"])
    cp(T.hb[:, 100:110], T.fi[:], ["fi"], ["hbt"])
    unwrap(6, T.hb[:, 100:110], ["hbt"])
    cp(T.ft[:], b[6][0:8, 0:B], ["b6"], ["ft"])
    dma("Y", T.yt[:], T.ft[:], ["ft"], [], "osn")
    g.wait_ge(T.sem.loc, sent[0])
    for s, v in tot.items():
        if know["P"].get(s, 0) < v:
            g.wait_ge(T.sem[s], v)
